import numpy as np
import ml_dtypes


def mxq(x, axis, fmt="e4m3"):
    dtype, down = {"e4m3": (ml_dtypes.float8_e4m3fn, 7), "e5m2": (ml_dtypes.float8_e5m2, 14)}[fmt]
    v = np.moveaxis(np.asarray(x, np.float32).astype(ml_dtypes.bfloat16).astype(np.float64), axis, -1)
    blocks = v.reshape(v.shape[:-1] + (-1, 32))
    amax = np.abs(blocks).max(-1, keepdims=True)
    byte = np.maximum(np.where(amax > 0, np.frexp(amax)[1] - 1 + 127, 0) - down, 1)
    scale = np.exp2(byte - 127.0)
    codes = (blocks / scale).astype(np.float32).astype(dtype).astype(np.float64)
    return np.moveaxis((codes * scale).reshape(v.shape), -1, axis)


WIDE = False


def mx_kscale(k):
    if not WIDE:
        return np.ones(k)
    levels = np.array([10, -10, 5, -5, 0])
    if k % 512:
        return np.exp2(np.random.permutation(np.resize(levels, k // 32))).repeat(32)
    a = np.empty((k // 512, 16))
    for p in range(k // 512):
        a[p, :8] = np.random.permutation(np.resize(levels, 8))
        for g in range(8):
            far = levels[np.abs(levels - a[p, g]) >= 10]
            a[p, g + 8] = far[np.random.randint(len(far))]
    return np.exp2(a.ravel()).repeat(32)


def f64(x):
    return np.asarray(x).astype(np.float64)


def striped(idx):
    return np.tile(idx.reshape(-1, 16).T, (8, 1)).astype(np.uint16)


def unstriped(offs):
    return offs[:16].T.reshape(-1).astype(np.int64)


def striped8(idx):
    return np.concatenate([x.reshape(-1, 16).T for x in idx]).astype(np.uint16)


def runs(offs, k):
    lists = np.stack([offs[16 * r : 16 * r + 16].T.reshape(-1) for r in range(8)]).astype(np.int64)
    return lists[np.arange(k) % 512 // 64]


def pack_weight(w):
    k, n = w.shape
    w = f64(np.asarray(w, np.float32).astype(ml_dtypes.bfloat16)).reshape(k // 32, 32, n)
    amax = np.abs(w).max(1)
    byte = np.clip(np.where(amax > 0, np.frexp(amax)[1] - 1 + 127 - 7, 1), 1, 254)
    scaled = (w * np.exp2(127.0 - byte)[:, None, :]).reshape(k, n).astype(np.float32)
    words = np.ascontiguousarray(scaled.reshape(k // 512, 128, 4, n).transpose(0, 1, 3, 2)).astype(ml_dtypes.float8_e4m3fn).view(np.uint8)
    return words, np.ascontiguousarray(byte.astype(np.uint8).reshape(k // 512, 16, n))


def unpack_weight(words, scales):
    g, p, n, _ = words.shape
    vals = np.ascontiguousarray(words).view(ml_dtypes.float8_e4m3fn).astype(np.float64) * np.repeat(np.exp2(scales.astype(np.float64) - 127.0), 8, axis=1)[..., None]
    return vals.transpose(0, 1, 3, 2).reshape(g * 512, n)


E2M1 = np.array([0.0, 0.5, 1.0, 1.5, 2.0, 3.0, 4.0, 6.0, -0.0, -0.5, -1.0, -1.5, -2.0, -3.0, -4.0, -6.0])


def pack_fp4(w):
    k, n = w.shape
    w = f64(np.asarray(w, np.float32).astype(ml_dtypes.bfloat16)).reshape(k // 32, 32, n)
    amax = np.abs(w).max(1)
    mant, ex = np.frexp(amax / 6.0)
    byte = np.clip(np.where(amax > 0, np.where(mant > 0.5, ex, ex - 1) + 127, 1), 1, 254)
    scaled = (w * np.exp2(127.0 - byte)[:, None, :]).reshape(k, n).astype(np.float32)
    c = np.ascontiguousarray(scaled.reshape(k // 512, 128, 4, n).transpose(0, 1, 3, 2)).astype(ml_dtypes.float4_e2m1fn).view(np.uint8) & 0xF
    words = (c[..., 0::2] | (c[..., 1::2] << 4)).reshape(k // 512, 128, 2 * n)
    return np.ascontiguousarray(words), np.ascontiguousarray(byte.astype(np.uint8).reshape(k // 512, 16, n))


def unpack_fp4(words, scales):
    g, _, n = scales.shape
    words = np.ascontiguousarray(words).reshape(g, 128, n, 2)
    nib = np.empty((g, 128, n, 4), np.uint8)
    nib[..., 0::2] = words & 0xF
    nib[..., 1::2] = words >> 4
    vals = E2M1[nib] * np.repeat(np.exp2(scales.astype(np.float64) - 127.0), 8, axis=1)[..., None]
    return vals.transpose(0, 1, 3, 2).reshape(g * 512, n)


def relu(v):
    return np.maximum(v, 0.0)

def planes(y):
    n, m = y.shape
    v = y.astype(np.float32).astype(ml_dtypes.bfloat16).astype(np.float64).reshape(n // 32, 32, m)
    top = np.abs(v).max(1)
    byte = np.clip(np.where(top > 0, np.frexp(top)[1] - 1 + 127 - 7, 1), 1, 254)
    codes = (v * np.exp2(127.0 - byte)[:, None, :]).reshape(n, m).astype(np.float32).astype(ml_dtypes.float8_e4m3fn).view(np.uint8)
    words = codes.reshape(n // 512, 128, 4, m).transpose(0, 1, 3, 2)
    return np.ascontiguousarray(words), np.ascontiguousarray(byte.astype(np.uint8).reshape(n // 512, 16, m))


K, T, S, V, N, H = 512, 2048, 512, 256, 512, 512


def setup_inputs():
    n = np.random.standard_normal
    s = mx_kscale(K)[:, None]
    u = mx_kscale(H)
    packed_xT = pack_weight(n((K, T)) * s)
    packed_w3 = pack_fp4(n((H, N)) / np.sqrt(H) / u[:, None])
    perm = np.stack([np.random.permutation(S) for _ in range(8)])
    return {
        "x_words": packed_xT[0],
        "x_scales": packed_xT[1],
        "w1": (n((K, H)) / np.sqrt(K) / s * u).astype(np.float32),
        "w2": (n((K, H)) / np.sqrt(K) / s * u).astype(np.float32),
        "wa": np.repeat(np.random.uniform(0.3, 1.2, (8, V)), 64, axis=0).astype(np.float32),
        "wb": np.repeat(np.random.uniform(0.3, 1.2, (8, V)), 64, axis=0).astype(np.float32),
        "w3_words": packed_w3[0],
        "w3_scales": packed_w3[1],
        "offs": striped(np.random.permutation(T)[:S]),
        "la": striped8(perm[:, :V]),
        "lb": striped8(perm[:, V:]),
    }


def reference(x_words, x_scales, w1, w2, wa, wb, w3_words, w3_scales, offs, la, lb):
    xq = unpack_weight(x_words, x_scales)[:, unstriped(offs)]
    e = mxq(f64(w2), 0, "e4m3").T @ xq
    b = (relu(e[np.arange(H)[:, None], runs(lb, H)])) * f64(wb)
    y = mxq(f64(w1), 0, "e4m3").T @ xq
    a = (relu(y[np.arange(H)[:, None], runs(la, H)])) * f64(wa)
    p = np.zeros((H, S))
    p[np.arange(H)[:, None], runs(la, H)] = a
    z = p.copy()
    z[np.arange(H)[:, None], runs(lb, H)] = b
    out_0 = unpack_fp4(w3_words, w3_scales).T @ mxq(z, 0, "e4m3")
    return (out_0,) + planes(out_0)

@@ -1,0 +1,177 @@
+from contextlib import ExitStack
+
+import concourse.mybir as mybir
+
+K, T, S, V, N, H = 512, 2048, 512, 256, 512, 512
+FLOPS = 2 * K * H * S * 2 + 2 * H * N * S
+
+F32 = mybir.dt.float32
+BF16 = mybir.dt.bfloat16
+I32 = mybir.dt.int32
+U32 = mybir.dt.uint32
+U16 = mybir.dt.uint16
+U8 = mybir.dt.uint8
+FP8X4 = mybir.dt.float8_e4m3fn_x4
+FP4X4 = mybir.dt.float4_e2m1fn_x4
+RELU = mybir.ActivationFunctionType.Relu
+MULT = mybir.AluOpType.mult
+
+P = 128
+PACK = 4
+CHUNK = 128
+
+
+def tile_picked_moe2w_relu_po_kernel(
+    tc, x_words, x_scales, w1, w2, wa, wb, w3_words, w3_scales, offs, la, lb, out_0, out_1, out_2
+):
+    nc = tc.nc
+    with ExitStack() as ctx:
+        lists = ctx.enter_context(tc.tile_pool(name="lists", bufs=1))
+        keep = ctx.enter_context(tc.tile_pool(name="keep", bufs=1))
+        ring = ctx.enter_context(tc.tile_pool(name="ring", bufs=3))
+        xs_pool = ctx.enter_context(tc.tile_pool(name="xs_pool", bufs=1))
+        xw_pool = ctx.enter_context(tc.tile_pool(name="xw_pool", bufs=1))
+        psum = ctx.enter_context(tc.psum_pool(name="psum", bufs=8))
+
+        offs_t = lists.tile([P, S // 16], U16, name="offs_t")
+        la_t = lists.tile([P, V // 16], U16, name="la_t")
+        lb_t = lists.tile([P, V // 16], U16, name="lb_t")
+
+        xs_all = xs_pool.tile([P, T], U8, name="xs_all", align_bytes=64, offset=0)
+        xw_all = xw_pool.tile([P, T], U32, name="xw_all", align_bytes=64, offset=0)
+        w1_raw = keep.tile([P, PACK, H], F32, name="w1_raw", tag="w_raw", align_bytes=64)
+        w3w_raw = keep.tile([P, 2 * N], U8, name="w3w_raw", align_bytes=64)
+        w3s_raw = keep.tile([P, N], U8, name="w3s_raw", align_bytes=64)
+
+        nc.vector.memset(xs_all[:].bitcast(I32), 0)
+        nc.gpsimd.memset(w3s_raw[:].bitcast(I32), 0)
+        nc.sync.dma_start(offs_t[:], offs)
+        nc.sync.dma_start(la_t[:], la)
+        nc.sync.dma_start(w1_raw[:], w1.rearrange("(p j) h -> p j h", j=PACK))
+        nc.sync.dma_start(lb_t[:], lb)
+        for q in range(4):
+            nc.scalar.dma_start(xs_all[32 * q : 32 * q + 4, :].bitcast(I32), x_scales[0, 4 * q : 4 * q + 4, :].bitcast(I32))
+        nc.sync.dma_start(xw_all[:].bitcast(I32), x_words[0].rearrange("p c r -> p (c r)").bitcast(I32))
+        for q in range(4):
+            nc.gpsimd.dma_start(w3s_raw[32 * q : 32 * q + 4, :].bitcast(I32), w3_scales[0, 4 * q : 4 * q + 4, :].bitcast(I32))
+        nc.sync.dma_start(w3w_raw[:].bitcast(I32), w3_words[0].bitcast(I32))
+
+        xs = keep.tile([P, S], U8, name="xs", align_bytes=64)
+        xw = keep.tile([P, S], U32, name="xw", align_bytes=64)
+        nc.vector.tensor_copy(xs[:], xs_all[:].indirect(offs_t[:]))
+        wa_t = xs_pool.tile([P, V], F32, name="wa_t", align_bytes=64, offset=0)
+        wb_t = xs_pool.tile([P, V], F32, name="wb_t", align_bytes=64, offset=4 * V)
+        nc.sync.dma_start(wa_t[:], wa.rearrange("(p j) v -> p j v", j=PACK)[:, 0, :])
+        nc.sync.dma_start(wb_t[:], wb.rearrange("(p j) v -> p j v", j=PACK)[:, 0, :])
+
+        def deal_weights(raw, dealt, m0, m1, copy):
+            copy(
+                dealt[:].rearrange("p (t m j) -> p m t j", t=PACK, j=PACK)[:, m0:m1],
+                raw[:].rearrange("p j (m t) -> p m t j", t=PACK)[:, m0:m1],
+            )
+
+        w1_dealt = keep.tile([P, PACK * H], BF16, name="w1_dealt", align_bytes=64)
+        w2_dealt = keep.tile([P, PACK * H], BF16, name="w2_dealt", tag="late", align_bytes=64)
+        w1_codes = keep.tile([P, H], U32, name="w1_codes", align_bytes=64)
+        w2_codes = keep.tile([P, H], U32, name="w2_codes", align_bytes=64)
+        w1_sc = keep.tile([P, H], U8, name="w1_sc", align_bytes=64)
+        w2_sc = keep.tile([P, H], U8, name="w2_sc", align_bytes=64)
+        deal_weights(w1_raw, w1_dealt, 0, 48, nc.scalar.copy)
+        deal_weights(w1_raw, w1_dealt, 48, P, nc.vector.tensor_copy)
+        w2_raw = keep.tile([P, PACK, H], F32, name="w2_raw", tag="w_raw", align_bytes=64)
+        nc.sync.dma_start(w2_raw[:], w2.rearrange("(p j) h -> p j h", j=PACK))
+        nc.vector.quantize_mx(w1_codes[:].bitcast(FP8X4), w1_sc[:], w1_dealt[:])
+        nc.vector.tensor_copy(xw[:], xw_all[:].indirect(offs_t[:]))
+
+        def first_layer(codes, scales, name):
+            tiles = []
+            for t in range(PACK):
+                cols = slice(t * P, (t + 1) * P)
+                acc = psum.tile([P, S], F32, name="acc", tag="acc")
+                nc.tensor.matmul_mx(acc[:], codes[:, cols].bitcast(FP8X4), scales[:, cols], xw[:].bitcast(FP8X4), xs[:], start=True, stop=True)
+                act = keep.tile([P, S], F32, name="%s%d" % (name, t), align_bytes=64)
+                nc.scalar.activation(act[:], acc[:], RELU)
+                tiles.append(act)
+            return tiles
+
+        relu_y = first_layer(w1_codes, w1_sc, "relu_y")
+
+        w3w = xw_pool.tile([P, 2 * N], U8, name="w3w", align_bytes=64, offset=0)
+        w3s = xw_pool.tile([P, N], U8, name="w3s", align_bytes=64, offset=2 * N)
+        nc.vector.tensor_copy(
+            w3w[:].rearrange("p (t m b) -> p m t b", t=PACK, b=2), w3w_raw[:].rearrange("p (m t b) -> p m t b", t=PACK, b=2)
+        )
+        nc.vector.tensor_copy(w3s[:].rearrange("p (t m) -> p m t", t=PACK), w3s_raw[:].rearrange("p (m t) -> p m t", t=PACK))
+
+        for m0 in range(0, P, 32):
+            deal_weights(w2_raw, w2_dealt, m0, m0 + 32, nc.scalar.copy)
+
+        z = [keep.tile([P, S], F32, name="z%d" % t, align_bytes=64) for t in range(PACK - 1)]
+        z_bf = keep.tile([P, S, PACK], BF16, name="z_bf", align_bytes=64)
+
+        def gather(src, idx):
+            picked = ring.tile([P, V], F32, name="picked", tag="picked")
+            nc.vector.tensor_copy(picked[:], src[:].indirect(idx[:]))
+            return picked
+
+        def scatter(t, picked, idx, weight):
+            nc.vector.tensor_tensor(z[t][:].indirect(idx[:]), picked[:], weight[:], MULT)
+
+        picked = gather(relu_y[0], la_t)
+        for t in range(PACK - 1):
+            ahead = gather(relu_y[t + 1], la_t)
+            scatter(t, picked, la_t, wa_t)
+            picked = ahead
+        nc.vector.quantize_mx(w2_codes[:].bitcast(FP8X4), w2_sc[:], w2_dealt[:])
+        relu_e = first_layer(w2_codes, w2_sc, "relu_e")
+        z.append(keep.tile([P, S], F32, name="z_last", tag="late", align_bytes=64))
+        scatter(PACK - 1, picked, la_t, wa_t)
+        picked = gather(relu_e[0], lb_t)
+        for t in range(PACK):
+            if t + 1 < PACK:
+                ahead = gather(relu_e[t + 1], lb_t)
+            scatter(t, picked, lb_t, wb_t)
+            picked = ahead
+            if t < 2:
+                nc.scalar.copy(z_bf[:, :, t], z[t][:])
+            if t == 2:
+                nc.scalar.copy(z_bf[:, : S // 2, 2:4], z[t][:, : S // 2].unsqueeze(2).to_broadcast([P, S // 2, 2]))
+                nc.scalar.copy(z_bf[:, S // 2 :, t], z[t][:, S // 2 :])
+
+        z_codes = keep.tile([P, S], U32, name="z_codes", align_bytes=64)
+        z_sc = keep.tile([P, S], U8, name="z_sc", align_bytes=64)
+        o_codes = keep.tile([P, S], U32, name="o_codes", align_bytes=64)
+        o_sc = keep.tile([P, S], U8, name="o_sc", align_bytes=64)
+        out_rows = out_0.rearrange("(p t) s -> p t s", t=PACK)
+        out_words = out_1[0].rearrange("p c r -> p (c r)").bitcast(I32)
+        chunks = [slice(c, c + CHUNK) for c in range(0, S, CHUNK)]
+        for c, cols in enumerate(chunks):
+            copy = nc.vector.tensor_copy if c < 2 else nc.scalar.copy
+            copy(z_bf[:, cols, PACK - 1], z[PACK - 1][:, cols])
+        for cols in (chunks[0], chunks[1], slice(S // 2, S)):
+            nc.vector.quantize_mx(z_codes[:, cols].bitcast(FP8X4), z_sc[:, cols], z_bf[:, cols, :].rearrange("p s t -> p (s t)"))
+        res_bf = keep.tile([P, S, PACK], BF16, name="res_bf", align_bytes=64)
+        for c, cols in enumerate(chunks):
+            acc = psum.tile([P, PACK, CHUNK], F32, name="acc", tag="acc")
+            for t in range(PACK):
+                nc.tensor.matmul_mx(
+                    acc[:, t, :],
+                    w3w[:, 2 * P * t : 2 * P * (t + 1)].bitcast(FP4X4),
+                    w3s[:, P * t : P * (t + 1)],
+                    z_codes[:, cols].bitcast(FP8X4),
+                    z_sc[:, cols],
+                    start=True,
+                    stop=True,
+                )
+            res = keep.tile([P, PACK, CHUNK], F32, name="res%d" % c, align_bytes=64)
+            nc.scalar.copy(res[:], acc[:])
+            nc.sync.dma_start(out_rows[:, :, cols], res[:])
+            nc.vector.tensor_copy(
+                res_bf[:, cols, :].rearrange("p (s i) t -> p s t i", i=4), res[:].rearrange("p t (s i) -> p s t i", i=4)
+            )
+        for cols in (slice(0, S // 2), chunks[2], chunks[3]):
+            nc.vector.quantize_mx(o_codes[:, cols].bitcast(FP8X4), o_sc[:, cols], res_bf[:, cols, :].rearrange("p s t -> p (s t)"))
+            nc.sync.dma_start(out_words[:, cols], o_codes[:, cols].bitcast(I32))
+        for q in range(4):
+            queue = nc.scalar if q < 3 else nc.sync
+            queue.dma_start(out_2[0, 4 * q : 4 * q + 4, :].bitcast(I32), o_sc[32 * q : 32 * q + 4, :].bitcast(I32))

@@ -29,7 +29,7 @@ def tile_picked_moe2w_relu_po_kernel(
         lists = ctx.enter_context(tc.tile_pool(name="lists", bufs=1))
         keep = ctx.enter_context(tc.tile_pool(name="keep", bufs=1))
         ring = ctx.enter_context(tc.tile_pool(name="ring", bufs=3))
-        xs_pool = ctx.enter_context(tc.tile_pool(name="xs_pool", bufs=1))
+        w1_pool = ctx.enter_context(tc.tile_pool(name="w1_pool", bufs=1))
         xw_pool = ctx.enter_context(tc.tile_pool(name="xw_pool", bufs=1))
         psum = ctx.enter_context(tc.psum_pool(name="psum", bufs=8))
 
@@ -37,74 +37,84 @@ def tile_picked_moe2w_relu_po_kernel(
         la_t = lists.tile([P, V // 16], U16, name="la_t")
         lb_t = lists.tile([P, V // 16], U16, name="lb_t")
 
-        xs_all = xs_pool.tile([P, T], U8, name="xs_all", align_bytes=64, offset=0)
+        xs_all = keep.tile([P, T], U8, name="xs_all", align_bytes=64)
         xw_all = xw_pool.tile([P, T], U32, name="xw_all", align_bytes=64, offset=0)
-        w1_raw = keep.tile([P, PACK, H], F32, name="w1_raw", tag="w_raw", align_bytes=64)
-        w3w_raw = keep.tile([P, 2 * N], U8, name="w3w_raw", align_bytes=64)
+        w1_lo = keep.tile([P, PACK, H // 2], F32, name="w1_lo", align_bytes=64)
+        w3w_raw = w1_pool.tile([P, 2 * N], U8, name="w3w_raw", align_bytes=64, offset=0)
         w3s_raw = keep.tile([P, N], U8, name="w3s_raw", align_bytes=64)
+        w1_rows = w1.rearrange("(p j) h -> p j h", j=PACK)
 
         nc.vector.memset(xs_all[:].bitcast(I32), 0)
         nc.gpsimd.memset(w3s_raw[:].bitcast(I32), 0)
         nc.sync.dma_start(offs_t[:], offs)
         nc.sync.dma_start(la_t[:], la)
-        nc.sync.dma_start(w1_raw[:], w1.rearrange("(p j) h -> p j h", j=PACK))
         nc.sync.dma_start(lb_t[:], lb)
+        nc.sync.dma_start(w3w_raw[:].bitcast(I32), w3_words[0].bitcast(I32))
+        nc.sync.dma_start(xw_all[:].bitcast(I32), x_words[0].rearrange("p c r -> p (c r)").bitcast(I32))
+        nc.sync.dma_start(w1_lo[:], w1_rows[:, :, : H // 2])
         for q in range(4):
             nc.scalar.dma_start(xs_all[32 * q : 32 * q + 4, :].bitcast(I32), x_scales[0, 4 * q : 4 * q + 4, :].bitcast(I32))
-        nc.sync.dma_start(xw_all[:].bitcast(I32), x_words[0].rearrange("p c r -> p (c r)").bitcast(I32))
         for q in range(4):
             nc.gpsimd.dma_start(w3s_raw[32 * q : 32 * q + 4, :].bitcast(I32), w3_scales[0, 4 * q : 4 * q + 4, :].bitcast(I32))
-        nc.sync.dma_start(w3w_raw[:].bitcast(I32), w3_words[0].bitcast(I32))
+
+        w3w = keep.tile([P, 2 * N], U8, name="w3w", align_bytes=64)
+        nc.vector.tensor_copy(
+            w3w[:].rearrange("p (t m b) -> p t m b", t=PACK, b=2), w3w_raw[:].rearrange("p (m t b) -> p t m b", t=PACK, b=2)
+        )
+        w1_hi = w1_pool.tile([P, PACK, H // 2], F32, name="w1_hi", align_bytes=64, offset=0)
+        nc.sync.dma_start(w1_hi[:], w1_rows[:, :, H // 2 :])
 
         xs = keep.tile([P, S], U8, name="xs", align_bytes=64)
         xw = keep.tile([P, S], U32, name="xw", align_bytes=64)
+        nc.vector.tensor_copy(xw[:], xw_all[:].indirect(offs_t[:]))
         nc.vector.tensor_copy(xs[:], xs_all[:].indirect(offs_t[:]))
-        wa_t = xs_pool.tile([P, V], F32, name="wa_t", align_bytes=64, offset=0)
-        wb_t = xs_pool.tile([P, V], F32, name="wb_t", align_bytes=64, offset=4 * V)
+        wa_t = xw_pool.tile([P, V], F32, name="wa_t", align_bytes=64, offset=0)
+        wb_t = xw_pool.tile([P, V], F32, name="wb_t", align_bytes=64, offset=4 * V)
+        w2_raw = xw_pool.tile([P, PACK, H], F32, name="w2_raw", align_bytes=64, offset=8 * V)
         nc.sync.dma_start(wa_t[:], wa.rearrange("(p j) v -> p j v", j=PACK)[:, 0, :])
         nc.sync.dma_start(wb_t[:], wb.rearrange("(p j) v -> p j v", j=PACK)[:, 0, :])
+        nc.sync.dma_start(w2_raw[:], w2.rearrange("(p j) h -> p j h", j=PACK))
 
-        def deal_weights(raw, dealt, m0, m1, copy):
+        def deal_weights(raw, first, dealt, m0, m1, copy):
             copy(
                 dealt[:].rearrange("p (t m j) -> p m t j", t=PACK, j=PACK)[:, m0:m1],
-                raw[:].rearrange("p j (m t) -> p m t j", t=PACK)[:, m0:m1],
+                raw[:].rearrange("p j (m t) -> p m t j", t=PACK)[:, m0 - first : m1 - first],
             )
 
-        w1_dealt = keep.tile([P, PACK * H], BF16, name="w1_dealt", align_bytes=64)
+        w1_dealt = keep.tile([P, PACK * H], BF16, name="w1_dealt", tag="w1_dealt", align_bytes=64)
         w2_dealt = keep.tile([P, PACK * H], BF16, name="w2_dealt", tag="late", align_bytes=64)
         w1_codes = keep.tile([P, H], U32, name="w1_codes", align_bytes=64)
         w2_codes = keep.tile([P, H], U32, name="w2_codes", align_bytes=64)
         w1_sc = keep.tile([P, H], U8, name="w1_sc", align_bytes=64)
         w2_sc = keep.tile([P, H], U8, name="w2_sc", align_bytes=64)
-        deal_weights(w1_raw, w1_dealt, 0, 48, nc.scalar.copy)
-        deal_weights(w1_raw, w1_dealt, 48, P, nc.vector.tensor_copy)
-        w2_raw = keep.tile([P, PACK, H], F32, name="w2_raw", tag="w_raw", align_bytes=64)
-        nc.sync.dma_start(w2_raw[:], w2.rearrange("(p j) h -> p j h", j=PACK))
-        nc.vector.quantize_mx(w1_codes[:].bitcast(FP8X4), w1_sc[:], w1_dealt[:])
-        nc.vector.tensor_copy(xw[:], xw_all[:].indirect(offs_t[:]))
+        deal_weights(w1_lo, 0, w1_dealt, 0, 64, nc.scalar.copy)
+        deal_weights(w1_hi, 64, w1_dealt, 64, 88, nc.scalar.copy)
+        deal_weights(w1_hi, 64, w1_dealt, 88, P, nc.vector.tensor_copy)
+        for c0, c1 in ((0, P), (P, 2 * P), (2 * P, H)):
+            nc.vector.quantize_mx(w1_codes[:, c0:c1].bitcast(FP8X4), w1_sc[:, c0:c1], w1_dealt[:, PACK * c0 : PACK * c1])
+        halves = (slice(0, S // 2), slice(S // 2, S))
 
-        def first_layer(codes, scales, name):
+        def first_layer(codes, scales, name, first_pieces):
             tiles = []
             for t in range(PACK):
                 cols = slice(t * P, (t + 1) * P)
-                acc = psum.tile([P, S], F32, name="acc", tag="acc")
-                nc.tensor.matmul_mx(acc[:], codes[:, cols].bitcast(FP8X4), scales[:, cols], xw[:].bitcast(FP8X4), xs[:], start=True, stop=True)
                 act = keep.tile([P, S], F32, name="%s%d" % (name, t), align_bytes=64)
-                nc.scalar.activation(act[:], acc[:], RELU)
+                for tokens in first_pieces if t == 0 else (slice(0, S),):
+                    acc = psum.tile([P, tokens.stop - tokens.start], F32, name="acc", tag="acc")
+                    nc.tensor.matmul_mx(
+                        acc[:], codes[:, cols].bitcast(FP8X4), scales[:, cols], xw[:, tokens].bitcast(FP8X4), xs[:, tokens], start=True, stop=True
+                    )
+                    nc.scalar.activation(act[:, tokens], acc[:], RELU)
                 tiles.append(act)
             return tiles
 
-        relu_y = first_layer(w1_codes, w1_sc, "relu_y")
+        relu_y = first_layer(w1_codes, w1_sc, "relu_y", halves)
 
-        w3w = xw_pool.tile([P, 2 * N], U8, name="w3w", align_bytes=64, offset=0)
-        w3s = xw_pool.tile([P, N], U8, name="w3s", align_bytes=64, offset=2 * N)
-        nc.vector.tensor_copy(
-            w3w[:].rearrange("p (t m b) -> p m t b", t=PACK, b=2), w3w_raw[:].rearrange("p (m t b) -> p m t b", t=PACK, b=2)
-        )
-        nc.vector.tensor_copy(w3s[:].rearrange("p (t m) -> p m t", t=PACK), w3s_raw[:].rearrange("p (m t) -> p m t", t=PACK))
+        w3s = keep.tile([P, N], U8, name="w3s", tag="w1_dealt", align_bytes=64)
+        nc.vector.tensor_copy(w3s[:].rearrange("p (t m) -> p t m", t=PACK), w3s_raw[:].rearrange("p (m t) -> p t m", t=PACK))
 
         for m0 in range(0, P, 32):
-            deal_weights(w2_raw, w2_dealt, m0, m0 + 32, nc.scalar.copy)
+            deal_weights(w2_raw, 0, w2_dealt, m0, m0 + 32, nc.scalar.copy)
 
         z = [keep.tile([P, S], F32, name="z%d" % t, align_bytes=64) for t in range(PACK - 1)]
         z_bf = keep.tile([P, S, PACK], BF16, name="z_bf", align_bytes=64)
@@ -123,7 +133,7 @@ def tile_picked_moe2w_relu_po_kernel(
             scatter(t, picked, la_t, wa_t)
             picked = ahead
         nc.vector.quantize_mx(w2_codes[:].bitcast(FP8X4), w2_sc[:], w2_dealt[:])
-        relu_e = first_layer(w2_codes, w2_sc, "relu_e")
+        relu_e = first_layer(w2_codes, w2_sc, "relu_e", (slice(0, S),))
         z.append(keep.tile([P, S], F32, name="z_last", tag="late", align_bytes=64))
         scatter(PACK - 1, picked, la_t, wa_t)
         picked = gather(relu_e[0], lb_t)
@@ -164,14 +174,17 @@ def tile_picked_moe2w_relu_po_kernel(
                     stop=True,
                 )
             res = keep.tile([P, PACK, CHUNK], F32, name="res%d" % c, align_bytes=64)
+            if c == len(chunks) - 1:
+                nc.vector.tensor_copy(res_bf[:, cols, :], acc[:].rearrange("p t s -> p s t"))
             nc.scalar.copy(res[:], acc[:])
             nc.sync.dma_start(out_rows[:, :, cols], res[:])
-            nc.vector.tensor_copy(
-                res_bf[:, cols, :].rearrange("p (s i) t -> p s t i", i=4), res[:].rearrange("p t (s i) -> p s t i", i=4)
-            )
+            if c < len(chunks) - 1:
+                nc.vector.tensor_copy(
+                    res_bf[:, cols, :].rearrange("p (s i) t -> p s t i", i=4), res[:].rearrange("p t (s i) -> p s t i", i=4)
+                )
         for cols in (slice(0, S // 2), chunks[2], chunks[3]):
             nc.vector.quantize_mx(o_codes[:, cols].bitcast(FP8X4), o_sc[:, cols], res_bf[:, cols, :].rearrange("p s t -> p (s t)"))
             nc.sync.dma_start(out_words[:, cols], o_codes[:, cols].bitcast(I32))
         for q in range(4):
-            queue = nc.scalar if q < 3 else nc.sync
+            queue = nc.scalar if q < 2 else nc.sync
             queue.dma_start(out_2[0, 4 * q : 4 * q + 4, :].bitcast(I32), o_sc[32 * q : 32 * q + 4, :].bitcast(I32))

@@ -1,6 +1,7 @@
 from contextlib import ExitStack
 
 import concourse.mybir as mybir
+from concourse.masks import make_identity
 
 K, T, S, V, N, H = 512, 2048, 512, 256, 512, 512
 FLOPS = 2 * K * H * S * 2 + 2 * H * N * S
@@ -46,12 +47,12 @@ def tile_picked_moe2w_relu_po_kernel(
 
         nc.vector.memset(xs_all[:].bitcast(I32), 0)
         nc.gpsimd.memset(w3s_raw[:].bitcast(I32), 0)
+        nc.sync.dma_start(w3w_raw[:].bitcast(I32), w3_words[0].bitcast(I32))
         nc.sync.dma_start(offs_t[:], offs)
         nc.sync.dma_start(la_t[:], la)
-        nc.sync.dma_start(lb_t[:], lb)
-        nc.sync.dma_start(w3w_raw[:].bitcast(I32), w3_words[0].bitcast(I32))
         nc.sync.dma_start(xw_all[:].bitcast(I32), x_words[0].rearrange("p c r -> p (c r)").bitcast(I32))
         nc.sync.dma_start(w1_lo[:], w1_rows[:, :, : H // 2])
+        nc.sync.dma_start(lb_t[:], lb)
         for q in range(4):
             nc.scalar.dma_start(xs_all[32 * q : 32 * q + 4, :].bitcast(I32), x_scales[0, 4 * q : 4 * q + 4, :].bitcast(I32))
         for q in range(4):
@@ -88,8 +89,8 @@ def tile_picked_moe2w_relu_po_kernel(
         w1_sc = keep.tile([P, H], U8, name="w1_sc", align_bytes=64)
         w2_sc = keep.tile([P, H], U8, name="w2_sc", align_bytes=64)
         deal_weights(w1_lo, 0, w1_dealt, 0, 64, nc.scalar.copy)
-        deal_weights(w1_hi, 64, w1_dealt, 64, 88, nc.scalar.copy)
-        deal_weights(w1_hi, 64, w1_dealt, 88, P, nc.vector.tensor_copy)
+        deal_weights(w1_hi, 64, w1_dealt, 64, 76, nc.scalar.copy)
+        deal_weights(w1_hi, 64, w1_dealt, 76, P, nc.vector.tensor_copy)
         for c0, c1 in ((0, P), (P, 2 * P), (2 * P, H)):
             nc.vector.quantize_mx(w1_codes[:, c0:c1].bitcast(FP8X4), w1_sc[:, c0:c1], w1_dealt[:, PACK * c0 : PACK * c1])
         halves = (slice(0, S // 2), slice(S // 2, S))
@@ -116,6 +117,8 @@ def tile_picked_moe2w_relu_po_kernel(
         for m0 in range(0, P, 32):
             deal_weights(w2_raw, 0, w2_dealt, m0, m0 + 32, nc.scalar.copy)
 
+        ident = keep.tile([P, P], F32, name="ident", align_bytes=64)
+        make_identity(nc, ident[:])
         z = [keep.tile([P, S], F32, name="z%d" % t, align_bytes=64) for t in range(PACK - 1)]
         z_bf = keep.tile([P, S, PACK], BF16, name="z_bf", align_bytes=64)
 
@@ -145,6 +148,12 @@ def tile_picked_moe2w_relu_po_kernel(
             if t < 2:
                 nc.scalar.copy(z_bf[:, :, t], z[t][:])
             if t == 2:
+                warm = psum.tile([P, S], F32, name="acc", tag="acc")
+                nc.tensor.transpose(warm[:, :P], z[t][:, :P], ident[:])
+                for u in range(3):
+                    nc.tensor.matmul_mx(
+                        warm[:], w2_codes[:, :P].bitcast(FP8X4), w2_sc[:, :P], xw[:].bitcast(FP8X4), xs[:], start=True, stop=True
+                    )
                 nc.scalar.copy(z_bf[:, : S // 2, 2:4], z[t][:, : S // 2].unsqueeze(2).to_broadcast([P, S // 2, 2]))
                 nc.scalar.copy(z_bf[:, S // 2 :, t], z[t][:, S // 2 :])
 
@@ -160,6 +169,7 @@ def tile_picked_moe2w_relu_po_kernel(
             copy(z_bf[:, cols, PACK - 1], z[PACK - 1][:, cols])
         for cols in (chunks[0], chunks[1], slice(S // 2, S)):
             nc.vector.quantize_mx(z_codes[:, cols].bitcast(FP8X4), z_sc[:, cols], z_bf[:, cols, :].rearrange("p s t -> p (s t)"))
+        accs = []
         res_bf = keep.tile([P, S, PACK], BF16, name="res_bf", align_bytes=64)
         for c, cols in enumerate(chunks):
             acc = psum.tile([P, PACK, CHUNK], F32, name="acc", tag="acc")
@@ -173,18 +183,30 @@ def tile_picked_moe2w_relu_po_kernel(
                     start=True,
                     stop=True,
                 )
-            res = keep.tile([P, PACK, CHUNK], F32, name="res%d" % c, align_bytes=64)
-            if c == len(chunks) - 1:
-                nc.vector.tensor_copy(res_bf[:, cols, :], acc[:].rearrange("p t s -> p s t"))
-            nc.scalar.copy(res[:], acc[:])
-            nc.sync.dma_start(out_rows[:, :, cols], res[:])
-            if c < len(chunks) - 1:
-                nc.vector.tensor_copy(
-                    res_bf[:, cols, :].rearrange("p (s i) t -> p s t i", i=4), res[:].rearrange("p t (s i) -> p s t i", i=4)
-                )
-        for cols in (slice(0, S // 2), chunks[2], chunks[3]):
+            accs.append(acc)
+
+        def interleave(cols, res):
+            nc.vector.tensor_copy(
+                res_bf[:, cols, :].rearrange("p (s i) t -> p s t i", i=4), res.rearrange("p t (s i) -> p s t i", i=4)
+            )
+
+        res0 = keep.tile([P, PACK, CHUNK], F32, name="res0", align_bytes=64)
+        res1 = keep.tile([P, PACK, CHUNK], F32, name="res1", align_bytes=64)
+        res23 = keep.tile([P, PACK, 2 * CHUNK], F32, name="res23", align_bytes=64)
+        nc.scalar.copy(res0[:], accs[0][:])
+        nc.sync.dma_start(out_rows[:, :, chunks[0]], res0[:])
+        nc.vector.tensor_copy(res1[:], accs[1][:])
+        nc.sync.dma_start(out_rows[:, :, chunks[1]], res1[:])
+        nc.scalar.copy(res23[:, :, :CHUNK], accs[2][:])
+        nc.scalar.copy(res23[:, :, CHUNK:], accs[3][:])
+        nc.sync.dma_start(out_rows[:, :, halves[1]], res23[:])
+        nc.scalar.copy(res_bf[:, chunks[3], :], accs[3][:].rearrange("p t s -> p s t"))
+        interleave(chunks[0], res0[:])
+        interleave(chunks[1], res1[:])
+        interleave(chunks[2], res23[:, :, :CHUNK])
+        for cols in halves:
             nc.vector.quantize_mx(o_codes[:, cols].bitcast(FP8X4), o_sc[:, cols], res_bf[:, cols, :].rearrange("p s t -> p (s t)"))
-            nc.sync.dma_start(out_words[:, cols], o_codes[:, cols].bitcast(I32))
+        nc.sync.dma_start(out_words, o_codes[:].bitcast(I32))
         for q in range(4):
             queue = nc.scalar if q < 2 else nc.sync
             queue.dma_start(out_2[0, 4 * q : 4 * q + 4, :].bitcast(I32), o_sc[32 * q : 32 * q + 4, :].bitcast(I32))

@@ -122,28 +122,28 @@ def tile_picked_moe2w_relu_po_kernel(
         z = [keep.tile([P, S], F32, name="z%d" % t, align_bytes=64) for t in range(PACK - 1)]
         z_bf = keep.tile([P, S, PACK], BF16, name="z_bf", align_bytes=64)
 
-        def gather(src, idx):
+        def gather(src, idx, weight):
             picked = ring.tile([P, V], F32, name="picked", tag="picked")
-            nc.vector.tensor_copy(picked[:], src[:].indirect(idx[:]))
+            nc.vector.tensor_tensor(picked[:], src[:].indirect(idx[:]), weight[:], MULT)
             return picked
 
-        def scatter(t, picked, idx, weight):
-            nc.vector.tensor_tensor(z[t][:].indirect(idx[:]), picked[:], weight[:], MULT)
+        def scatter(t, picked, idx):
+            nc.vector.tensor_copy(z[t][:].indirect(idx[:]), picked[:])
 
-        picked = gather(relu_y[0], la_t)
+        picked = gather(relu_y[0], la_t, wa_t)
         for t in range(PACK - 1):
-            ahead = gather(relu_y[t + 1], la_t)
-            scatter(t, picked, la_t, wa_t)
+            ahead = gather(relu_y[t + 1], la_t, wa_t)
+            scatter(t, picked, la_t)
             picked = ahead
         nc.vector.quantize_mx(w2_codes[:].bitcast(FP8X4), w2_sc[:], w2_dealt[:])
         relu_e = first_layer(w2_codes, w2_sc, "relu_e", (slice(0, S),))
         z.append(keep.tile([P, S], F32, name="z_last", tag="late", align_bytes=64))
-        scatter(PACK - 1, picked, la_t, wa_t)
-        picked = gather(relu_e[0], lb_t)
+        scatter(PACK - 1, picked, la_t)
+        picked = gather(relu_e[0], lb_t, wb_t)
         for t in range(PACK):
             if t + 1 < PACK:
-                ahead = gather(relu_e[t + 1], lb_t)
-            scatter(t, picked, lb_t, wb_t)
+                ahead = gather(relu_e[t + 1], lb_t, wb_t)
+            scatter(t, picked, lb_t)
             picked = ahead
             if t < 2:
                 nc.scalar.copy(z_bf[:, :, t], z[t][:])

@@ -30,28 +30,27 @@ def tile_picked_moe2w_relu_po_kernel(
         lists = ctx.enter_context(tc.tile_pool(name="lists", bufs=1))
         keep = ctx.enter_context(tc.tile_pool(name="keep", bufs=1))
         ring = ctx.enter_context(tc.tile_pool(name="ring", bufs=3))
+        xs_pool = ctx.enter_context(tc.tile_pool(name="xs_pool", bufs=1))
         w1_pool = ctx.enter_context(tc.tile_pool(name="w1_pool", bufs=1))
         xw_pool = ctx.enter_context(tc.tile_pool(name="xw_pool", bufs=1))
+        z_pool = ctx.enter_context(tc.tile_pool(name="z_pool", bufs=1))
         psum = ctx.enter_context(tc.psum_pool(name="psum", bufs=8))
 
         offs_t = lists.tile([P, S // 16], U16, name="offs_t")
         la_t = lists.tile([P, V // 16], U16, name="la_t")
         lb_t = lists.tile([P, V // 16], U16, name="lb_t")
 
-        xs_all = keep.tile([P, T], U8, name="xs_all", align_bytes=64)
+        xs_all = xs_pool.tile([P, T], U8, name="xs_all", align_bytes=64, offset=2048)
         xw_all = xw_pool.tile([P, T], U32, name="xw_all", align_bytes=64, offset=0)
-        w1_lo = keep.tile([P, PACK, H // 2], F32, name="w1_lo", align_bytes=64)
         w3w_raw = w1_pool.tile([P, 2 * N], U8, name="w3w_raw", align_bytes=64, offset=0)
         w3s_raw = keep.tile([P, N], U8, name="w3s_raw", align_bytes=64)
-        w1_rows = w1.rearrange("(p j) h -> p j h", j=PACK)
 
         nc.vector.memset(xs_all[:].bitcast(I32), 0)
         nc.gpsimd.memset(w3s_raw[:].bitcast(I32), 0)
         nc.sync.dma_start(w3w_raw[:].bitcast(I32), w3_words[0].bitcast(I32))
         nc.sync.dma_start(offs_t[:], offs)
-        nc.sync.dma_start(la_t[:], la)
         nc.sync.dma_start(xw_all[:].bitcast(I32), x_words[0].rearrange("p c r -> p (c r)").bitcast(I32))
-        nc.sync.dma_start(w1_lo[:], w1_rows[:, :, : H // 2])
+        nc.sync.dma_start(la_t[:], la)
         nc.sync.dma_start(lb_t[:], lb)
         for q in range(4):
             nc.scalar.dma_start(xs_all[32 * q : 32 * q + 4, :].bitcast(I32), x_scales[0, 4 * q : 4 * q + 4, :].bitcast(I32))
@@ -62,64 +61,69 @@ def tile_picked_moe2w_relu_po_kernel(
         nc.vector.tensor_copy(
             w3w[:].rearrange("p (t m b) -> p t m b", t=PACK, b=2), w3w_raw[:].rearrange("p (m t b) -> p t m b", t=PACK, b=2)
         )
-        w1_hi = w1_pool.tile([P, PACK, H // 2], F32, name="w1_hi", align_bytes=64, offset=0)
-        nc.sync.dma_start(w1_hi[:], w1_rows[:, :, H // 2 :])
+        w1_raw = w1_pool.tile([P, PACK, H], F32, name="w1_raw", align_bytes=64, offset=0)
+        nc.sync.dma_start(w1_raw[:], w1.rearrange("(p j) h -> p j h", j=PACK))
 
         xs = keep.tile([P, S], U8, name="xs", align_bytes=64)
-        xw = keep.tile([P, S], U32, name="xw", align_bytes=64)
-        nc.vector.tensor_copy(xw[:], xw_all[:].indirect(offs_t[:]))
         nc.vector.tensor_copy(xs[:], xs_all[:].indirect(offs_t[:]))
-        wa_t = xw_pool.tile([P, V], F32, name="wa_t", align_bytes=64, offset=0)
-        wb_t = xw_pool.tile([P, V], F32, name="wb_t", align_bytes=64, offset=4 * V)
-        w2_raw = xw_pool.tile([P, PACK, H], F32, name="w2_raw", align_bytes=64, offset=8 * V)
+        xw = xs_pool.tile([P, S], U32, name="xw", align_bytes=64, offset=512)
+        wa_t = xs_pool.tile([P, V], F32, name="wa_t", align_bytes=64, offset=2560)
+        w2_raw = xs_pool.tile([P, PACK, H], F32, name="w2_raw", align_bytes=64, offset=3584)
+        nc.vector.tensor_copy(xw[:], xw_all[:].indirect(offs_t[:]))
         nc.sync.dma_start(wa_t[:], wa.rearrange("(p j) v -> p j v", j=PACK)[:, 0, :])
-        nc.sync.dma_start(wb_t[:], wb.rearrange("(p j) v -> p j v", j=PACK)[:, 0, :])
         nc.sync.dma_start(w2_raw[:], w2.rearrange("(p j) h -> p j h", j=PACK))
+        wb_t = xw_pool.tile([P, V], F32, name="wb_t", align_bytes=64, offset=0)
+        nc.sync.dma_start(wb_t[:], wb.rearrange("(p j) v -> p j v", j=PACK)[:, 0, :])
 
-        def deal_weights(raw, first, dealt, m0, m1, copy):
+        def deal_weights(raw, dealt, ms, ts, copy):
             copy(
-                dealt[:].rearrange("p (t m j) -> p m t j", t=PACK, j=PACK)[:, m0:m1],
-                raw[:].rearrange("p j (m t) -> p m t j", t=PACK)[:, m0 - first : m1 - first],
+                dealt[:].rearrange("p (t m j) -> p m t j", t=PACK, j=PACK)[:, ms, ts],
+                raw[:].rearrange("p j (m t) -> p m t j", t=PACK)[:, ms, ts],
             )
 
         w1_dealt = keep.tile([P, PACK * H], BF16, name="w1_dealt", tag="w1_dealt", align_bytes=64)
-        w2_dealt = keep.tile([P, PACK * H], BF16, name="w2_dealt", tag="late", align_bytes=64)
+        w2_dealt = z_pool.tile([P, PACK * H], BF16, name="w2_dealt", align_bytes=64, offset=0)
         w1_codes = keep.tile([P, H], U32, name="w1_codes", align_bytes=64)
         w2_codes = keep.tile([P, H], U32, name="w2_codes", align_bytes=64)
         w1_sc = keep.tile([P, H], U8, name="w1_sc", align_bytes=64)
         w2_sc = keep.tile([P, H], U8, name="w2_sc", align_bytes=64)
-        deal_weights(w1_lo, 0, w1_dealt, 0, 64, nc.scalar.copy)
-        deal_weights(w1_hi, 64, w1_dealt, 64, 76, nc.scalar.copy)
-        deal_weights(w1_hi, 64, w1_dealt, 76, P, nc.vector.tensor_copy)
-        for c0, c1 in ((0, P), (P, 2 * P), (2 * P, H)):
+
+        def quantize_w1(c0, c1):
             nc.vector.quantize_mx(w1_codes[:, c0:c1].bitcast(FP8X4), w1_sc[:, c0:c1], w1_dealt[:, PACK * c0 : PACK * c1])
+
+        first, rest = slice(0, 1), slice(1, PACK)
+        deal_weights(w1_raw, w1_dealt, slice(0, 42), first, nc.scalar.copy)
+        deal_weights(w1_raw, w1_dealt, slice(42, P), first, nc.vector.tensor_copy)
+        quantize_w1(0, P)
+        deal_weights(w1_raw, w1_dealt, slice(0, 64), rest, nc.scalar.copy)
+        deal_weights(w1_raw, w1_dealt, slice(64, 80), rest, nc.vector.tensor_copy)
+        deal_weights(w1_raw, w1_dealt, slice(80, P), rest, nc.vector.tensor_copy)
+        quantize_w1(P, 2 * P)
+        quantize_w1(2 * P, H)
         halves = (slice(0, S // 2), slice(S // 2, S))
 
-        def first_layer(codes, scales, name, first_pieces):
-            tiles = []
-            for t in range(PACK):
+        def first_layer(codes, scales, tiles, order, first_pieces):
+            for t in order:
                 cols = slice(t * P, (t + 1) * P)
-                act = keep.tile([P, S], F32, name="%s%d" % (name, t), align_bytes=64)
-                for tokens in first_pieces if t == 0 else (slice(0, S),):
+                for tokens in first_pieces if t == order[0] else (slice(0, S),):
                     acc = psum.tile([P, tokens.stop - tokens.start], F32, name="acc", tag="acc")
                     nc.tensor.matmul_mx(
                         acc[:], codes[:, cols].bitcast(FP8X4), scales[:, cols], xw[:, tokens].bitcast(FP8X4), xs[:, tokens], start=True, stop=True
                     )
-                    nc.scalar.activation(act[:, tokens], acc[:], RELU)
-                tiles.append(act)
-            return tiles
+                    nc.scalar.activation(tiles[t][:, tokens], acc[:], RELU)
 
-        relu_y = first_layer(w1_codes, w1_sc, "relu_y", halves)
+        relu_y = [z_pool.tile([P, S], F32, name="relu_y%d" % t, align_bytes=64, offset=4096 + 2048 * t) for t in range(PACK)]
+        relu_e = [keep.tile([P, S], F32, name="relu_e%d" % t, align_bytes=64) for t in range(PACK)]
+        first_layer(w1_codes, w1_sc, relu_y, (0, 1, 2, 3), halves)
 
         w3s = keep.tile([P, N], U8, name="w3s", tag="w1_dealt", align_bytes=64)
         nc.vector.tensor_copy(w3s[:].rearrange("p (t m) -> p t m", t=PACK), w3s_raw[:].rearrange("p (m t) -> p t m", t=PACK))
 
         for m0 in range(0, P, 32):
-            deal_weights(w2_raw, 0, w2_dealt, m0, m0 + 32, nc.scalar.copy)
+            deal_weights(w2_raw, w2_dealt, slice(m0, m0 + 32), slice(0, PACK), nc.scalar.copy)
 
         ident = keep.tile([P, P], F32, name="ident", align_bytes=64)
         make_identity(nc, ident[:])
-        z = [keep.tile([P, S], F32, name="z%d" % t, align_bytes=64) for t in range(PACK - 1)]
         z_bf = keep.tile([P, S, PACK], BF16, name="z_bf", align_bytes=64)
 
         def gather(src, idx, weight):
@@ -130,15 +134,18 @@ def tile_picked_moe2w_relu_po_kernel(
         def scatter(t, picked, idx):
             nc.vector.tensor_copy(z[t][:].indirect(idx[:]), picked[:])
 
+        z_at = (12288, 14336, 0, 2048)
+        z = []
         picked = gather(relu_y[0], la_t, wa_t)
-        for t in range(PACK - 1):
-            ahead = gather(relu_y[t + 1], la_t, wa_t)
+        for t in range(PACK):
+            if t + 1 < PACK:
+                ahead = gather(relu_y[t + 1], la_t, wa_t)
+            if t == 2:
+                nc.vector.quantize_mx(w2_codes[:].bitcast(FP8X4), w2_sc[:], w2_dealt[:])
+                first_layer(w2_codes, w2_sc, relu_e, (3, 2, 1, 0), (slice(0, S),))
+            z.append(z_pool.tile([P, S], F32, name="z%d" % t, align_bytes=64, offset=z_at[t]))
             scatter(t, picked, la_t)
             picked = ahead
-        nc.vector.quantize_mx(w2_codes[:].bitcast(FP8X4), w2_sc[:], w2_dealt[:])
-        relu_e = first_layer(w2_codes, w2_sc, "relu_e", (slice(0, S),))
-        z.append(keep.tile([P, S], F32, name="z_last", tag="late", align_bytes=64))
-        scatter(PACK - 1, picked, la_t)
         picked = gather(relu_e[0], lb_t, wb_t)
         for t in range(PACK):
             if t + 1 < PACK:

@@ -30,8 +30,6 @@ def tile_picked_moe2w_relu_po_kernel(
         lists = ctx.enter_context(tc.tile_pool(name="lists", bufs=1))
         keep = ctx.enter_context(tc.tile_pool(name="keep", bufs=1))
         ring = ctx.enter_context(tc.tile_pool(name="ring", bufs=3))
-        xs_pool = ctx.enter_context(tc.tile_pool(name="xs_pool", bufs=1))
-        w1_pool = ctx.enter_context(tc.tile_pool(name="w1_pool", bufs=1))
         xw_pool = ctx.enter_context(tc.tile_pool(name="xw_pool", bufs=1))
         z_pool = ctx.enter_context(tc.tile_pool(name="z_pool", bufs=1))
         psum = ctx.enter_context(tc.psum_pool(name="psum", bufs=8))
@@ -40,45 +38,54 @@ def tile_picked_moe2w_relu_po_kernel(
         la_t = lists.tile([P, V // 16], U16, name="la_t")
         lb_t = lists.tile([P, V // 16], U16, name="lb_t")
 
-        xs_all = xs_pool.tile([P, T], U8, name="xs_all", align_bytes=64, offset=2048)
+        xs_all = keep.tile([P, T], U8, name="xs_all", align_bytes=64)
+        xs = keep.tile([P, S], U8, name="xs", align_bytes=64)
         xw_all = xw_pool.tile([P, T], U32, name="xw_all", align_bytes=64, offset=0)
-        w3w_raw = w1_pool.tile([P, 2 * N], U8, name="w3w_raw", align_bytes=64, offset=0)
+        w1_lo = keep.tile([P, PACK, H // 2], F32, name="w1_lo", align_bytes=64)
+        w1_hi = keep.tile([P, PACK, H // 2], F32, name="w1_hi", align_bytes=64)
+        w1_rows = w1.rearrange("(p j) h -> p j h", j=PACK)
+        w3w_raw = keep.tile([P, 2 * N], U8, name="w3w_raw", align_bytes=64)
         w3s_raw = keep.tile([P, N], U8, name="w3s_raw", align_bytes=64)
 
-        nc.vector.memset(xs_all[:].bitcast(I32), 0)
+        nc.vector.memset(xs_all[64:, :].bitcast(I32), 0)
+        nc.vector.memset(xs_all[32:64, :].bitcast(I32), 0)
+        nc.vector.memset(xs[:].bitcast(I32), 0)
         nc.gpsimd.memset(w3s_raw[:].bitcast(I32), 0)
-        nc.sync.dma_start(w3w_raw[:].bitcast(I32), w3_words[0].bitcast(I32))
+        for r in (0, 16):
+            nc.sync.dma_start(xs_all[r : r + 16, :].bitcast(I32), x_scales[0].bitcast(I32))
         nc.sync.dma_start(offs_t[:], offs)
+        nc.sync.dma_start(w3w_raw[:].bitcast(I32), w3_words[0].bitcast(I32))
         nc.sync.dma_start(xw_all[:].bitcast(I32), x_words[0].rearrange("p c r -> p (c r)").bitcast(I32))
+        nc.sync.dma_start(w1_lo[:], w1_rows[:, :, : H // 2])
+        nc.sync.dma_start(w1_hi[:], w1_rows[:, :, H // 2 :])
         nc.sync.dma_start(la_t[:], la)
         nc.sync.dma_start(lb_t[:], lb)
         for q in range(4):
-            nc.scalar.dma_start(xs_all[32 * q : 32 * q + 4, :].bitcast(I32), x_scales[0, 4 * q : 4 * q + 4, :].bitcast(I32))
-        for q in range(4):
             nc.gpsimd.dma_start(w3s_raw[32 * q : 32 * q + 4, :].bitcast(I32), w3_scales[0, 4 * q : 4 * q + 4, :].bitcast(I32))
+
+        xs_rows = keep.tile([P, S], U8, name="xs_rows", align_bytes=64)
+        nc.vector.tensor_copy(xs_rows[:], xs_all[:].indirect(offs_t[:]))
+        for q in range(4):
+            nc.sync.dma_start(xs[32 * q : 32 * q + 4, :].bitcast(I32), xs_rows[4 * q : 4 * q + 4, :].bitcast(I32))
 
         w3w = keep.tile([P, 2 * N], U8, name="w3w", align_bytes=64)
         nc.vector.tensor_copy(
             w3w[:].rearrange("p (t m b) -> p t m b", t=PACK, b=2), w3w_raw[:].rearrange("p (m t b) -> p t m b", t=PACK, b=2)
         )
-        w1_raw = w1_pool.tile([P, PACK, H], F32, name="w1_raw", align_bytes=64, offset=0)
-        nc.sync.dma_start(w1_raw[:], w1.rearrange("(p j) h -> p j h", j=PACK))
 
-        xs = keep.tile([P, S], U8, name="xs", align_bytes=64)
-        nc.vector.tensor_copy(xs[:], xs_all[:].indirect(offs_t[:]))
-        xw = xs_pool.tile([P, S], U32, name="xw", align_bytes=64, offset=512)
-        wa_t = xs_pool.tile([P, V], F32, name="wa_t", align_bytes=64, offset=2560)
-        w2_raw = xs_pool.tile([P, PACK, H], F32, name="w2_raw", align_bytes=64, offset=3584)
+        xw = keep.tile([P, S], U32, name="xw", align_bytes=64)
         nc.vector.tensor_copy(xw[:], xw_all[:].indirect(offs_t[:]))
+        wa_t = xw_pool.tile([P, V], F32, name="wa_t", align_bytes=64, offset=0)
+        w2_raw = xw_pool.tile([P, PACK, H], F32, name="w2_raw", align_bytes=64, offset=8 * V)
+        wb_t = xw_pool.tile([P, V], F32, name="wb_t", align_bytes=64, offset=4 * V)
         nc.sync.dma_start(wa_t[:], wa.rearrange("(p j) v -> p j v", j=PACK)[:, 0, :])
         nc.sync.dma_start(w2_raw[:], w2.rearrange("(p j) h -> p j h", j=PACK))
-        wb_t = xw_pool.tile([P, V], F32, name="wb_t", align_bytes=64, offset=0)
         nc.sync.dma_start(wb_t[:], wb.rearrange("(p j) v -> p j v", j=PACK)[:, 0, :])
 
-        def deal_weights(raw, dealt, ms, ts, copy):
+        def deal_weights(raw, dealt, ms, ts, copy, first=0):
             copy(
                 dealt[:].rearrange("p (t m j) -> p m t j", t=PACK, j=PACK)[:, ms, ts],
-                raw[:].rearrange("p j (m t) -> p m t j", t=PACK)[:, ms, ts],
+                raw[:].rearrange("p j (m t) -> p m t j", t=PACK)[:, ms.start - first : ms.stop - first, ts],
             )
 
         w1_dealt = keep.tile([P, PACK * H], BF16, name="w1_dealt", tag="w1_dealt", align_bytes=64)
@@ -91,13 +98,11 @@ def tile_picked_moe2w_relu_po_kernel(
         def quantize_w1(c0, c1):
             nc.vector.quantize_mx(w1_codes[:, c0:c1].bitcast(FP8X4), w1_sc[:, c0:c1], w1_dealt[:, PACK * c0 : PACK * c1])
 
-        first, rest = slice(0, 1), slice(1, PACK)
-        deal_weights(w1_raw, w1_dealt, slice(0, 42), first, nc.scalar.copy)
-        deal_weights(w1_raw, w1_dealt, slice(42, P), first, nc.vector.tensor_copy)
+        deal_weights(w1_lo, w1_dealt, slice(0, 40), slice(0, PACK), nc.scalar.copy)
+        deal_weights(w1_lo, w1_dealt, slice(40, 64), slice(0, PACK), nc.vector.tensor_copy)
+        deal_weights(w1_hi, w1_dealt, slice(64, P), slice(0, 1), nc.vector.tensor_copy, 64)
         quantize_w1(0, P)
-        deal_weights(w1_raw, w1_dealt, slice(0, 64), rest, nc.scalar.copy)
-        deal_weights(w1_raw, w1_dealt, slice(64, 80), rest, nc.vector.tensor_copy)
-        deal_weights(w1_raw, w1_dealt, slice(80, P), rest, nc.vector.tensor_copy)
+        deal_weights(w1_hi, w1_dealt, slice(64, P), slice(1, PACK), nc.scalar.copy, 64)
         quantize_w1(P, 2 * P)
         quantize_w1(2 * P, H)
         halves = (slice(0, S // 2), slice(S // 2, S))
@@ -112,7 +117,7 @@ def tile_picked_moe2w_relu_po_kernel(
                     )
                     nc.scalar.activation(tiles[t][:, tokens], acc[:], RELU)
 
-        relu_y = [z_pool.tile([P, S], F32, name="relu_y%d" % t, align_bytes=64, offset=4096 + 2048 * t) for t in range(PACK)]
+        relu_y = [keep.tile([P, S], F32, name="relu_y%d" % t, align_bytes=64) for t in range(PACK)]
         relu_e = [keep.tile([P, S], F32, name="relu_e%d" % t, align_bytes=64) for t in range(PACK)]
         first_layer(w1_codes, w1_sc, relu_y, (0, 1, 2, 3), halves)
 
@@ -134,7 +139,7 @@ def tile_picked_moe2w_relu_po_kernel(
         def scatter(t, picked, idx):
             nc.vector.tensor_copy(z[t][:].indirect(idx[:]), picked[:])
 
-        z_at = (12288, 14336, 0, 2048)
+        z_at = (4096, 6144, 0, 2048)
         z = []
         picked = gather(relu_y[0], la_t, wa_t)
         for t in range(PACK):

@@ -1,7 +1,6 @@
 from contextlib import ExitStack
 
 import concourse.mybir as mybir
-from concourse.masks import make_identity
 
 K, T, S, V, N, H = 512, 2048, 512, 256, 512, 512
 FLOPS = 2 * K * H * S * 2 + 2 * H * N * S
@@ -38,21 +37,19 @@ def tile_picked_moe2w_relu_po_kernel(
         la_t = lists.tile([P, V // 16], U16, name="la_t")
         lb_t = lists.tile([P, V // 16], U16, name="lb_t")
 
-        xs_all = keep.tile([P, T], U8, name="xs_all", align_bytes=64)
+        xs_all = keep.tile([P, T], U8, name="xs_all", tag="xs_all", align_bytes=64)
         xs = keep.tile([P, S], U8, name="xs", align_bytes=64)
         xw_all = xw_pool.tile([P, T], U32, name="xw_all", align_bytes=64, offset=0)
         w1_lo = keep.tile([P, PACK, H // 2], F32, name="w1_lo", align_bytes=64)
         w1_hi = keep.tile([P, PACK, H // 2], F32, name="w1_hi", align_bytes=64)
         w1_rows = w1.rearrange("(p j) h -> p j h", j=PACK)
         w3w_raw = keep.tile([P, 2 * N], U8, name="w3w_raw", align_bytes=64)
-        w3s_raw = keep.tile([P, N], U8, name="w3s_raw", align_bytes=64)
 
         nc.vector.memset(xs_all[64:, :].bitcast(I32), 0)
         nc.vector.memset(xs_all[32:64, :].bitcast(I32), 0)
         nc.vector.memset(xs[:].bitcast(I32), 0)
-        nc.gpsimd.memset(w3s_raw[:].bitcast(I32), 0)
-        for r in (0, 16):
-            nc.sync.dma_start(xs_all[r : r + 16, :].bitcast(I32), x_scales[0].bitcast(I32))
+        nc.sync.dma_start(xs_all[:16, :].bitcast(I32), x_scales[0].bitcast(I32))
+        nc.scalar.dma_start(xs_all[16:32, :].bitcast(I32), x_scales[0].bitcast(I32))
         nc.sync.dma_start(offs_t[:], offs)
         nc.sync.dma_start(w3w_raw[:].bitcast(I32), w3_words[0].bitcast(I32))
         nc.sync.dma_start(xw_all[:].bitcast(I32), x_words[0].rearrange("p c r -> p (c r)").bitcast(I32))
@@ -60,13 +57,15 @@ def tile_picked_moe2w_relu_po_kernel(
         nc.sync.dma_start(w1_hi[:], w1_rows[:, :, H // 2 :])
         nc.sync.dma_start(la_t[:], la)
         nc.sync.dma_start(lb_t[:], lb)
-        for q in range(4):
-            nc.gpsimd.dma_start(w3s_raw[32 * q : 32 * q + 4, :].bitcast(I32), w3_scales[0, 4 * q : 4 * q + 4, :].bitcast(I32))
 
         xs_rows = keep.tile([P, S], U8, name="xs_rows", align_bytes=64)
         nc.vector.tensor_copy(xs_rows[:], xs_all[:].indirect(offs_t[:]))
         for q in range(4):
             nc.sync.dma_start(xs[32 * q : 32 * q + 4, :].bitcast(I32), xs_rows[4 * q : 4 * q + 4, :].bitcast(I32))
+
+        w3s_raw = keep.tile([P, N], U8, name="w3s_raw", tag="xs_all", align_bytes=64)
+        nc.gpsimd.memset(w3s_raw[:].bitcast(I32), 0)
+        nc.sync.dma_start(w3s_raw[:16, :].bitcast(I32), w3_scales[0].bitcast(I32))
 
         w3w = keep.tile([P, 2 * N], U8, name="w3w", align_bytes=64)
         nc.vector.tensor_copy(
@@ -98,14 +97,16 @@ def tile_picked_moe2w_relu_po_kernel(
         def quantize_w1(c0, c1):
             nc.vector.quantize_mx(w1_codes[:, c0:c1].bitcast(FP8X4), w1_sc[:, c0:c1], w1_dealt[:, PACK * c0 : PACK * c1])
 
-        deal_weights(w1_lo, w1_dealt, slice(0, 40), slice(0, PACK), nc.scalar.copy)
-        deal_weights(w1_lo, w1_dealt, slice(40, 64), slice(0, PACK), nc.vector.tensor_copy)
+        deal_weights(w1_lo, w1_dealt, slice(0, 48), slice(0, PACK), nc.scalar.copy)
+        deal_weights(w1_lo, w1_dealt, slice(48, 64), slice(0, PACK), nc.vector.tensor_copy)
         deal_weights(w1_hi, w1_dealt, slice(64, P), slice(0, 1), nc.vector.tensor_copy, 64)
         quantize_w1(0, P)
         deal_weights(w1_hi, w1_dealt, slice(64, P), slice(1, PACK), nc.scalar.copy, 64)
         quantize_w1(P, 2 * P)
         quantize_w1(2 * P, H)
         halves = (slice(0, S // 2), slice(S // 2, S))
+        w3s_rows = keep.tile([P, N], U8, name="w3s_rows", align_bytes=64)
+        nc.vector.tensor_copy(w3s_rows[:].rearrange("p (t m) -> p t m", t=PACK), w3s_raw[:].rearrange("p (m t) -> p t m", t=PACK))
 
         def first_layer(codes, scales, tiles, order, first_pieces):
             for t in order:
@@ -121,18 +122,14 @@ def tile_picked_moe2w_relu_po_kernel(
         relu_e = [keep.tile([P, S], F32, name="relu_e%d" % t, align_bytes=64) for t in range(PACK)]
         first_layer(w1_codes, w1_sc, relu_y, (0, 1, 2, 3), halves)
 
-        w3s = keep.tile([P, N], U8, name="w3s", tag="w1_dealt", align_bytes=64)
-        nc.vector.tensor_copy(w3s[:].rearrange("p (t m) -> p t m", t=PACK), w3s_raw[:].rearrange("p (m t) -> p t m", t=PACK))
 
         for m0 in range(0, P, 32):
             deal_weights(w2_raw, w2_dealt, slice(m0, m0 + 32), slice(0, PACK), nc.scalar.copy)
 
-        ident = keep.tile([P, P], F32, name="ident", align_bytes=64)
-        make_identity(nc, ident[:])
         z_bf = keep.tile([P, S, PACK], BF16, name="z_bf", align_bytes=64)
 
         def gather(src, idx, weight):
-            picked = ring.tile([P, V], F32, name="picked", tag="picked")
+            picked = ring.tile([P, V], F32, name="picked", tag="picked", align_bytes=64)
             nc.vector.tensor_tensor(picked[:], src[:].indirect(idx[:]), weight[:], MULT)
             return picked
 
@@ -147,7 +144,7 @@ def tile_picked_moe2w_relu_po_kernel(
                 ahead = gather(relu_y[t + 1], la_t, wa_t)
             if t == 2:
                 nc.vector.quantize_mx(w2_codes[:].bitcast(FP8X4), w2_sc[:], w2_dealt[:])
-                first_layer(w2_codes, w2_sc, relu_e, (3, 2, 1, 0), (slice(0, S),))
+                first_layer(w2_codes, w2_sc, relu_e, (1, 0, 2, 3), (slice(0, S),))
             z.append(z_pool.tile([P, S], F32, name="z%d" % t, align_bytes=64, offset=z_at[t]))
             scatter(t, picked, la_t)
             picked = ahead
@@ -155,17 +152,21 @@ def tile_picked_moe2w_relu_po_kernel(
         for t in range(PACK):
             if t + 1 < PACK:
                 ahead = gather(relu_e[t + 1], lb_t, wb_t)
+            if t == PACK - 2:
+                w3s = ring.tile([P, N], U8, name="w3s", tag="picked", align_bytes=64)
+                nc.gpsimd.memset(w3s[:].bitcast(I32), 0)
+                for q in range(4):
+                    nc.sync.dma_start(w3s[32 * q : 32 * q + 4, :].bitcast(I32), w3s_rows[4 * q : 4 * q + 4, :].bitcast(I32))
+                warm = psum.tile([P, S], F32, name="acc", tag="acc")
+                for u in range(2):
+                    nc.tensor.matmul_mx(
+                        warm[:], w3w[:, : 2 * P].bitcast(FP4X4), w3s[:, :P], xw[:].bitcast(FP8X4), xs[:], start=True, stop=True
+                    )
             scatter(t, picked, lb_t)
             picked = ahead
             if t < 2:
                 nc.scalar.copy(z_bf[:, :, t], z[t][:])
             if t == 2:
-                warm = psum.tile([P, S], F32, name="acc", tag="acc")
-                nc.tensor.transpose(warm[:, :P], z[t][:, :P], ident[:])
-                for u in range(3):
-                    nc.tensor.matmul_mx(
-                        warm[:], w2_codes[:, :P].bitcast(FP8X4), w2_sc[:, :P], xw[:].bitcast(FP8X4), xs[:], start=True, stop=True
-                    )
                 nc.scalar.copy(z_bf[:, : S // 2, 2:4], z[t][:, : S // 2].unsqueeze(2).to_broadcast([P, S // 2, 2]))
                 nc.scalar.copy(z_bf[:, S // 2 :, t], z[t][:, S // 2 :])
 
@@ -181,13 +182,13 @@ def tile_picked_moe2w_relu_po_kernel(
             copy(z_bf[:, cols, PACK - 1], z[PACK - 1][:, cols])
         for cols in (chunks[0], chunks[1], slice(S // 2, S)):
             nc.vector.quantize_mx(z_codes[:, cols].bitcast(FP8X4), z_sc[:, cols], z_bf[:, cols, :].rearrange("p s t -> p (s t)"))
-        accs = []
         res_bf = keep.tile([P, S, PACK], BF16, name="res_bf", align_bytes=64)
-        for c, cols in enumerate(chunks):
-            acc = psum.tile([P, PACK, CHUNK], F32, name="acc", tag="acc")
-            for t in range(PACK):
+
+        def second_layer(cols, slots):
+            acc = psum.tile([P, len(slots), CHUNK], F32, name="acc", tag="acc")
+            for i, t in enumerate(slots):
                 nc.tensor.matmul_mx(
-                    acc[:, t, :],
+                    acc[:, i, :],
                     w3w[:, 2 * P * t : 2 * P * (t + 1)].bitcast(FP4X4),
                     w3s[:, P * t : P * (t + 1)],
                     z_codes[:, cols].bitcast(FP8X4),
@@ -195,30 +196,38 @@ def tile_picked_moe2w_relu_po_kernel(
                     start=True,
                     stop=True,
                 )
-            accs.append(acc)
+            return acc
+
+        acc0_lo = second_layer(chunks[0], (0, 1))
+        acc0_hi = second_layer(chunks[0], (2, 3))
+        accs = [None] + [second_layer(cols, range(PACK)) for cols in chunks[1:]]
 
         def interleave(cols, res):
             nc.vector.tensor_copy(
                 res_bf[:, cols, :].rearrange("p (s i) t -> p s t i", i=4), res.rearrange("p t (s i) -> p s t i", i=4)
             )
 
+        def quantize_out(cols):
+            nc.vector.quantize_mx(o_codes[:, cols].bitcast(FP8X4), o_sc[:, cols], res_bf[:, cols, :].rearrange("p s t -> p (s t)"))
+            nc.sync.dma_start(out_words[:, cols], o_codes[:, cols].bitcast(I32))
+
         res0 = keep.tile([P, PACK, CHUNK], F32, name="res0", align_bytes=64)
         res1 = keep.tile([P, PACK, CHUNK], F32, name="res1", align_bytes=64)
         res23 = keep.tile([P, PACK, 2 * CHUNK], F32, name="res23", align_bytes=64)
-        nc.scalar.copy(res0[:], accs[0][:])
+        nc.scalar.copy(res0[:, :2], acc0_lo[:])
+        nc.vector.tensor_copy(res0[:, 2:], acc0_hi[:])
         nc.sync.dma_start(out_rows[:, :, chunks[0]], res0[:])
-        nc.vector.tensor_copy(res1[:], accs[1][:])
+        nc.scalar.copy(res1[:], accs[1][:])
         nc.sync.dma_start(out_rows[:, :, chunks[1]], res1[:])
-        nc.scalar.copy(res23[:, :, :CHUNK], accs[2][:])
+        nc.vector.tensor_copy(res23[:, :, :CHUNK], accs[2][:])
         nc.scalar.copy(res23[:, :, CHUNK:], accs[3][:])
         nc.sync.dma_start(out_rows[:, :, halves[1]], res23[:])
         nc.scalar.copy(res_bf[:, chunks[3], :], accs[3][:].rearrange("p t s -> p s t"))
         interleave(chunks[0], res0[:])
         interleave(chunks[1], res1[:])
+        quantize_out(halves[0])
         interleave(chunks[2], res23[:, :, :CHUNK])
-        for cols in halves:
-            nc.vector.quantize_mx(o_codes[:, cols].bitcast(FP8X4), o_sc[:, cols], res_bf[:, cols, :].rearrange("p s t -> p (s t)"))
-        nc.sync.dma_start(out_words, o_codes[:].bitcast(I32))
+        quantize_out(halves[1])
         for q in range(4):
             queue = nc.scalar if q < 2 else nc.sync
             queue.dma_start(out_2[0, 4 * q : 4 * q + 4, :].bitcast(I32), o_sc[32 * q : 32 * q + 4, :].bitcast(I32))

@@ -29,6 +29,7 @@ def tile_picked_moe2w_relu_po_kernel(
         lists = ctx.enter_context(tc.tile_pool(name="lists", bufs=1))
         keep = ctx.enter_context(tc.tile_pool(name="keep", bufs=1))
         ring = ctx.enter_context(tc.tile_pool(name="ring", bufs=3))
+        xs_pool = ctx.enter_context(tc.tile_pool(name="xs_pool", bufs=1))
         xw_pool = ctx.enter_context(tc.tile_pool(name="xw_pool", bufs=1))
         z_pool = ctx.enter_context(tc.tile_pool(name="z_pool", bufs=1))
         psum = ctx.enter_context(tc.psum_pool(name="psum", bufs=8))
@@ -37,11 +38,11 @@ def tile_picked_moe2w_relu_po_kernel(
         la_t = lists.tile([P, V // 16], U16, name="la_t")
         lb_t = lists.tile([P, V // 16], U16, name="lb_t")
 
-        xs_all = keep.tile([P, T], U8, name="xs_all", tag="xs_all", align_bytes=64)
+        xs_all = xs_pool.tile([P, T], U8, name="xs_all", align_bytes=64, offset=0)
         xs = keep.tile([P, S], U8, name="xs", align_bytes=64)
         xw_all = xw_pool.tile([P, T], U32, name="xw_all", align_bytes=64, offset=0)
-        w1_lo = keep.tile([P, PACK, H // 2], F32, name="w1_lo", align_bytes=64)
-        w1_hi = keep.tile([P, PACK, H // 2], F32, name="w1_hi", align_bytes=64)
+        w1_lo = keep.tile([P, 2, H], F32, name="w1_lo", align_bytes=64)
+        w1_hi = keep.tile([P, 2, H], F32, name="w1_hi", align_bytes=64)
         w1_rows = w1.rearrange("(p j) h -> p j h", j=PACK)
         w3w_raw = keep.tile([P, 2 * N], U8, name="w3w_raw", align_bytes=64)
 
@@ -51,11 +52,11 @@ def tile_picked_moe2w_relu_po_kernel(
         nc.sync.dma_start(xs_all[:16, :].bitcast(I32), x_scales[0].bitcast(I32))
         nc.scalar.dma_start(xs_all[16:32, :].bitcast(I32), x_scales[0].bitcast(I32))
         nc.sync.dma_start(offs_t[:], offs)
+        nc.sync.dma_start(la_t[:], la)
         nc.sync.dma_start(w3w_raw[:].bitcast(I32), w3_words[0].bitcast(I32))
         nc.sync.dma_start(xw_all[:].bitcast(I32), x_words[0].rearrange("p c r -> p (c r)").bitcast(I32))
-        nc.sync.dma_start(w1_lo[:], w1_rows[:, :, : H // 2])
-        nc.sync.dma_start(w1_hi[:], w1_rows[:, :, H // 2 :])
-        nc.sync.dma_start(la_t[:], la)
+        nc.sync.dma_start(w1_lo[:], w1_rows[:, :2])
+        nc.sync.dma_start(w1_hi[:], w1_rows[:, 2:])
         nc.sync.dma_start(lb_t[:], lb)
 
         xs_rows = keep.tile([P, S], U8, name="xs_rows", align_bytes=64)
@@ -63,7 +64,9 @@ def tile_picked_moe2w_relu_po_kernel(
         for q in range(4):
             nc.sync.dma_start(xs[32 * q : 32 * q + 4, :].bitcast(I32), xs_rows[4 * q : 4 * q + 4, :].bitcast(I32))
 
-        w3s_raw = keep.tile([P, N], U8, name="w3s_raw", tag="xs_all", align_bytes=64)
+        wa_t = xs_pool.tile([P, V], F32, name="wa_t", align_bytes=64, offset=0)
+        nc.sync.dma_start(wa_t[:], wa.rearrange("(p j) v -> p j v", j=PACK)[:, 0, :])
+        w3s_raw = xs_pool.tile([P, N], U8, name="w3s_raw", align_bytes=64, offset=4 * V)
         nc.gpsimd.memset(w3s_raw[:].bitcast(I32), 0)
         nc.sync.dma_start(w3s_raw[:16, :].bitcast(I32), w3_scales[0].bitcast(I32))
 
@@ -74,17 +77,15 @@ def tile_picked_moe2w_relu_po_kernel(
 
         xw = keep.tile([P, S], U32, name="xw", align_bytes=64)
         nc.vector.tensor_copy(xw[:], xw_all[:].indirect(offs_t[:]))
-        wa_t = xw_pool.tile([P, V], F32, name="wa_t", align_bytes=64, offset=0)
         w2_raw = xw_pool.tile([P, PACK, H], F32, name="w2_raw", align_bytes=64, offset=8 * V)
         wb_t = xw_pool.tile([P, V], F32, name="wb_t", align_bytes=64, offset=4 * V)
-        nc.sync.dma_start(wa_t[:], wa.rearrange("(p j) v -> p j v", j=PACK)[:, 0, :])
         nc.sync.dma_start(w2_raw[:], w2.rearrange("(p j) h -> p j h", j=PACK))
         nc.sync.dma_start(wb_t[:], wb.rearrange("(p j) v -> p j v", j=PACK)[:, 0, :])
 
-        def deal_weights(raw, dealt, ms, ts, copy, first=0):
+        def deal_weights(raw, dealt, ms, ts, copy, js=slice(0, PACK)):
             copy(
-                dealt[:].rearrange("p (t m j) -> p m t j", t=PACK, j=PACK)[:, ms, ts],
-                raw[:].rearrange("p j (m t) -> p m t j", t=PACK)[:, ms.start - first : ms.stop - first, ts],
+                dealt[:].rearrange("p (t m j) -> p m t j", t=PACK, j=PACK)[:, ms, ts, js],
+                raw[:].rearrange("p j (m t) -> p m t j", t=PACK)[:, ms, ts],
             )
 
         w1_dealt = keep.tile([P, PACK * H], BF16, name="w1_dealt", tag="w1_dealt", align_bytes=64)
@@ -97,11 +98,12 @@ def tile_picked_moe2w_relu_po_kernel(
         def quantize_w1(c0, c1):
             nc.vector.quantize_mx(w1_codes[:, c0:c1].bitcast(FP8X4), w1_sc[:, c0:c1], w1_dealt[:, PACK * c0 : PACK * c1])
 
-        deal_weights(w1_lo, w1_dealt, slice(0, 48), slice(0, PACK), nc.scalar.copy)
-        deal_weights(w1_lo, w1_dealt, slice(48, 64), slice(0, PACK), nc.vector.tensor_copy)
-        deal_weights(w1_hi, w1_dealt, slice(64, P), slice(0, 1), nc.vector.tensor_copy, 64)
+        deal_weights(w1_lo, w1_dealt, slice(0, 88), slice(0, PACK), nc.scalar.copy, slice(0, 2))
+        deal_weights(w1_lo, w1_dealt, slice(88, P), slice(0, PACK), nc.vector.tensor_copy, slice(0, 2))
+        deal_weights(w1_hi, w1_dealt, slice(0, P), slice(0, 1), nc.vector.tensor_copy, slice(2, PACK))
         quantize_w1(0, P)
-        deal_weights(w1_hi, w1_dealt, slice(64, P), slice(1, PACK), nc.scalar.copy, 64)
+        deal_weights(w1_hi, w1_dealt, slice(0, 96), slice(1, PACK), nc.scalar.copy, slice(2, PACK))
+        deal_weights(w1_hi, w1_dealt, slice(96, P), slice(1, PACK), nc.vector.tensor_copy, slice(2, PACK))
         quantize_w1(P, 2 * P)
         quantize_w1(2 * P, H)
         halves = (slice(0, S // 2), slice(S // 2, S))

@@ -18,7 +18,12 @@ MULT = mybir.AluOpType.mult
 
 P = 128
 PACK = 4
+BLOCKS = 16
 CHUNK = 128
+W1_EARLY_SHARE = 88
+W1_LATE_SHARE = 96
+W2_STEP = 32
+WARM_PASSES = 2
 
 
 def tile_picked_moe2w_relu_po_kernel(
@@ -46,11 +51,15 @@ def tile_picked_moe2w_relu_po_kernel(
         w1_rows = w1.rearrange("(p j) h -> p j h", j=PACK)
         w3w_raw = keep.tile([P, 2 * N], U8, name="w3w_raw", align_bytes=64)
 
+        def move_to_plane(plane, rows):
+            for q in range(4):
+                nc.sync.dma_start(plane[32 * q : 32 * q + 4, :].bitcast(I32), rows[4 * q : 4 * q + 4, :].bitcast(I32))
+
         nc.vector.memset(xs_all[64:, :].bitcast(I32), 0)
         nc.vector.memset(xs_all[32:64, :].bitcast(I32), 0)
         nc.vector.memset(xs[:].bitcast(I32), 0)
-        nc.sync.dma_start(xs_all[:16, :].bitcast(I32), x_scales[0].bitcast(I32))
-        nc.scalar.dma_start(xs_all[16:32, :].bitcast(I32), x_scales[0].bitcast(I32))
+        nc.sync.dma_start(xs_all[:BLOCKS, :].bitcast(I32), x_scales[0].bitcast(I32))
+        nc.scalar.dma_start(xs_all[BLOCKS : 2 * BLOCKS, :].bitcast(I32), x_scales[0].bitcast(I32))
         nc.sync.dma_start(offs_t[:], offs)
         nc.sync.dma_start(la_t[:], la)
         nc.sync.dma_start(w3w_raw[:].bitcast(I32), w3_words[0].bitcast(I32))
@@ -61,14 +70,13 @@ def tile_picked_moe2w_relu_po_kernel(
 
         xs_rows = keep.tile([P, S], U8, name="xs_rows", align_bytes=64)
         nc.vector.tensor_copy(xs_rows[:], xs_all[:].indirect(offs_t[:]))
-        for q in range(4):
-            nc.sync.dma_start(xs[32 * q : 32 * q + 4, :].bitcast(I32), xs_rows[4 * q : 4 * q + 4, :].bitcast(I32))
+        move_to_plane(xs, xs_rows)
 
         wa_t = xs_pool.tile([P, V], F32, name="wa_t", align_bytes=64, offset=0)
         nc.sync.dma_start(wa_t[:], wa.rearrange("(p j) v -> p j v", j=PACK)[:, 0, :])
         w3s_raw = xs_pool.tile([P, N], U8, name="w3s_raw", align_bytes=64, offset=4 * V)
         nc.gpsimd.memset(w3s_raw[:].bitcast(I32), 0)
-        nc.sync.dma_start(w3s_raw[:16, :].bitcast(I32), w3_scales[0].bitcast(I32))
+        nc.sync.dma_start(w3s_raw[:BLOCKS, :].bitcast(I32), w3_scales[0].bitcast(I32))
 
         w3w = keep.tile([P, 2 * N], U8, name="w3w", align_bytes=64)
         nc.vector.tensor_copy(
@@ -88,7 +96,7 @@ def tile_picked_moe2w_relu_po_kernel(
                 raw[:].rearrange("p j (m t) -> p m t j", t=PACK)[:, ms, ts],
             )
 
-        w1_dealt = keep.tile([P, PACK * H], BF16, name="w1_dealt", tag="w1_dealt", align_bytes=64)
+        w1_dealt = keep.tile([P, PACK * H], BF16, name="w1_dealt", align_bytes=64)
         w2_dealt = z_pool.tile([P, PACK * H], BF16, name="w2_dealt", align_bytes=64, offset=0)
         w1_codes = keep.tile([P, H], U32, name="w1_codes", align_bytes=64)
         w2_codes = keep.tile([P, H], U32, name="w2_codes", align_bytes=64)
@@ -98,12 +106,14 @@ def tile_picked_moe2w_relu_po_kernel(
         def quantize_w1(c0, c1):
             nc.vector.quantize_mx(w1_codes[:, c0:c1].bitcast(FP8X4), w1_sc[:, c0:c1], w1_dealt[:, PACK * c0 : PACK * c1])
 
-        deal_weights(w1_lo, w1_dealt, slice(0, 88), slice(0, PACK), nc.scalar.copy, slice(0, 2))
-        deal_weights(w1_lo, w1_dealt, slice(88, P), slice(0, PACK), nc.vector.tensor_copy, slice(0, 2))
-        deal_weights(w1_hi, w1_dealt, slice(0, P), slice(0, 1), nc.vector.tensor_copy, slice(2, PACK))
+        every_t, first_t, later_t = slice(0, PACK), slice(0, 1), slice(1, PACK)
+        lo_slots, hi_slots = slice(0, 2), slice(2, PACK)
+        deal_weights(w1_lo, w1_dealt, slice(0, W1_EARLY_SHARE), every_t, nc.scalar.copy, lo_slots)
+        deal_weights(w1_lo, w1_dealt, slice(W1_EARLY_SHARE, P), every_t, nc.vector.tensor_copy, lo_slots)
+        deal_weights(w1_hi, w1_dealt, slice(0, P), first_t, nc.vector.tensor_copy, hi_slots)
         quantize_w1(0, P)
-        deal_weights(w1_hi, w1_dealt, slice(0, 96), slice(1, PACK), nc.scalar.copy, slice(2, PACK))
-        deal_weights(w1_hi, w1_dealt, slice(96, P), slice(1, PACK), nc.vector.tensor_copy, slice(2, PACK))
+        deal_weights(w1_hi, w1_dealt, slice(0, W1_LATE_SHARE), later_t, nc.scalar.copy, hi_slots)
+        deal_weights(w1_hi, w1_dealt, slice(W1_LATE_SHARE, P), later_t, nc.vector.tensor_copy, hi_slots)
         quantize_w1(P, 2 * P)
         quantize_w1(2 * P, H)
         halves = (slice(0, S // 2), slice(S // 2, S))
@@ -124,9 +134,8 @@ def tile_picked_moe2w_relu_po_kernel(
         relu_e = [keep.tile([P, S], F32, name="relu_e%d" % t, align_bytes=64) for t in range(PACK)]
         first_layer(w1_codes, w1_sc, relu_y, (0, 1, 2, 3), halves)
 
-
-        for m0 in range(0, P, 32):
-            deal_weights(w2_raw, w2_dealt, slice(m0, m0 + 32), slice(0, PACK), nc.scalar.copy)
+        for m0 in range(0, P, W2_STEP):
+            deal_weights(w2_raw, w2_dealt, slice(m0, m0 + W2_STEP), every_t, nc.scalar.copy)
 
         z_bf = keep.tile([P, S, PACK], BF16, name="z_bf", align_bytes=64)
 
@@ -138,7 +147,6 @@ def tile_picked_moe2w_relu_po_kernel(
         def scatter(t, picked, idx):
             nc.vector.tensor_copy(z[t][:].indirect(idx[:]), picked[:])
 
-        z_at = (4096, 6144, 0, 2048)
         z = []
         picked = gather(relu_y[0], la_t, wa_t)
         for t in range(PACK):
@@ -147,20 +155,19 @@ def tile_picked_moe2w_relu_po_kernel(
             if t == 2:
                 nc.vector.quantize_mx(w2_codes[:].bitcast(FP8X4), w2_sc[:], w2_dealt[:])
                 first_layer(w2_codes, w2_sc, relu_e, (1, 0, 2, 3), (slice(0, S),))
-            z.append(z_pool.tile([P, S], F32, name="z%d" % t, align_bytes=64, offset=z_at[t]))
+            z.append(z_pool.tile([P, S], F32, name="z%d" % t, align_bytes=64, offset=4 * S * ((t + 2) % PACK)))
             scatter(t, picked, la_t)
             picked = ahead
         picked = gather(relu_e[0], lb_t, wb_t)
         for t in range(PACK):
             if t + 1 < PACK:
                 ahead = gather(relu_e[t + 1], lb_t, wb_t)
-            if t == PACK - 2:
+            if t == 2:
                 w3s = ring.tile([P, N], U8, name="w3s", tag="picked", align_bytes=64)
                 nc.gpsimd.memset(w3s[:].bitcast(I32), 0)
-                for q in range(4):
-                    nc.sync.dma_start(w3s[32 * q : 32 * q + 4, :].bitcast(I32), w3s_rows[4 * q : 4 * q + 4, :].bitcast(I32))
+                move_to_plane(w3s, w3s_rows)
                 warm = psum.tile([P, S], F32, name="acc", tag="acc")
-                for u in range(2):
+                for u in range(WARM_PASSES):
                     nc.tensor.matmul_mx(
                         warm[:], w3w[:, : 2 * P].bitcast(FP4X4), w3s[:, :P], xw[:].bitcast(FP8X4), xs[:], start=True, stop=True
                     )
@@ -182,13 +189,13 @@ def tile_picked_moe2w_relu_po_kernel(
         for c, cols in enumerate(chunks):
             copy = nc.vector.tensor_copy if c < 2 else nc.scalar.copy
             copy(z_bf[:, cols, PACK - 1], z[PACK - 1][:, cols])
-        for cols in (chunks[0], chunks[1], slice(S // 2, S)):
+        for cols in chunks:
             nc.vector.quantize_mx(z_codes[:, cols].bitcast(FP8X4), z_sc[:, cols], z_bf[:, cols, :].rearrange("p s t -> p (s t)"))
         res_bf = keep.tile([P, S, PACK], BF16, name="res_bf", align_bytes=64)
 
-        def second_layer(cols, slots):
-            acc = psum.tile([P, len(slots), CHUNK], F32, name="acc", tag="acc")
-            for i, t in enumerate(slots):
+        def second_layer(cols, tiles):
+            acc = psum.tile([P, len(tiles), CHUNK], F32, name="acc", tag="acc")
+            for i, t in enumerate(tiles):
                 nc.tensor.matmul_mx(
                     acc[:, i, :],
                     w3w[:, 2 * P * t : 2 * P * (t + 1)].bitcast(FP4X4),
@@ -202,7 +209,7 @@ def tile_picked_moe2w_relu_po_kernel(
 
         acc0_lo = second_layer(chunks[0], (0, 1))
         acc0_hi = second_layer(chunks[0], (2, 3))
-        accs = [None] + [second_layer(cols, range(PACK)) for cols in chunks[1:]]
+        acc1, acc2, acc3 = [second_layer(cols, range(PACK)) for cols in chunks[1:]]
 
         def interleave(cols, res):
             nc.vector.tensor_copy(
@@ -211,6 +218,8 @@ def tile_picked_moe2w_relu_po_kernel(
 
         def quantize_out(cols):
             nc.vector.quantize_mx(o_codes[:, cols].bitcast(FP8X4), o_sc[:, cols], res_bf[:, cols, :].rearrange("p s t -> p (s t)"))
+
+        def store_words(cols):
             nc.sync.dma_start(out_words[:, cols], o_codes[:, cols].bitcast(I32))
 
         res0 = keep.tile([P, PACK, CHUNK], F32, name="res0", align_bytes=64)
@@ -219,17 +228,20 @@ def tile_picked_moe2w_relu_po_kernel(
         nc.scalar.copy(res0[:, :2], acc0_lo[:])
         nc.vector.tensor_copy(res0[:, 2:], acc0_hi[:])
         nc.sync.dma_start(out_rows[:, :, chunks[0]], res0[:])
-        nc.scalar.copy(res1[:], accs[1][:])
+        nc.scalar.copy(res1[:], acc1[:])
         nc.sync.dma_start(out_rows[:, :, chunks[1]], res1[:])
-        nc.vector.tensor_copy(res23[:, :, :CHUNK], accs[2][:])
-        nc.scalar.copy(res23[:, :, CHUNK:], accs[3][:])
+        nc.vector.tensor_copy(res23[:, :, :CHUNK], acc2[:])
+        nc.scalar.copy(res23[:, :, CHUNK:], acc3[:])
         nc.sync.dma_start(out_rows[:, :, halves[1]], res23[:])
-        nc.scalar.copy(res_bf[:, chunks[3], :], accs[3][:].rearrange("p t s -> p s t"))
+        nc.scalar.copy(res_bf[:, chunks[3], :], acc3[:].rearrange("p t s -> p s t"))
         interleave(chunks[0], res0[:])
         interleave(chunks[1], res1[:])
-        quantize_out(halves[0])
         interleave(chunks[2], res23[:, :, :CHUNK])
-        quantize_out(halves[1])
+        quantize_out(halves[0])
+        quantize_out(chunks[2])
+        store_words(slice(0, 3 * CHUNK))
+        quantize_out(chunks[3])
+        store_words(chunks[3])
         for q in range(4):
             queue = nc.scalar if q < 2 else nc.sync
             queue.dma_start(out_2[0, 4 * q : 4 * q + 4, :].bitcast(I32), o_sc[32 * q : 32 * q + 4, :].bitcast(I32))

@@ -20,10 +20,10 @@ P = 128
 PACK = 4
 BLOCKS = 16
 CHUNK = 128
-W1_EARLY_SHARE = 88
-W1_LATE_SHARE = 96
+ROWS_AT = P - BLOCKS
+W1_SHARE = 44
 W2_STEP = 32
-WARM_PASSES = 2
+WARM_PASSES = 3
 
 
 def tile_picked_moe2w_relu_po_kernel(
@@ -34,8 +34,9 @@ def tile_picked_moe2w_relu_po_kernel(
         lists = ctx.enter_context(tc.tile_pool(name="lists", bufs=1))
         keep = ctx.enter_context(tc.tile_pool(name="keep", bufs=1))
         ring = ctx.enter_context(tc.tile_pool(name="ring", bufs=3))
-        xs_pool = ctx.enter_context(tc.tile_pool(name="xs_pool", bufs=1))
+        w_pool = ctx.enter_context(tc.tile_pool(name="w_pool", bufs=1))
         xw_pool = ctx.enter_context(tc.tile_pool(name="xw_pool", bufs=1))
+        d_pool = ctx.enter_context(tc.tile_pool(name="d_pool", bufs=1))
         z_pool = ctx.enter_context(tc.tile_pool(name="z_pool", bufs=1))
         psum = ctx.enter_context(tc.psum_pool(name="psum", bufs=8))
 
@@ -43,99 +44,98 @@ def tile_picked_moe2w_relu_po_kernel(
         la_t = lists.tile([P, V // 16], U16, name="la_t")
         lb_t = lists.tile([P, V // 16], U16, name="lb_t")
 
-        xs_all = xs_pool.tile([P, T], U8, name="xs_all", align_bytes=64, offset=0)
+        xs_all = keep.tile([P, T], U8, name="xs_all", align_bytes=64)
         xs = keep.tile([P, S], U8, name="xs", align_bytes=64)
         xw_all = xw_pool.tile([P, T], U32, name="xw_all", align_bytes=64, offset=0)
-        w1_lo = keep.tile([P, 2, H], F32, name="w1_lo", align_bytes=64)
-        w1_hi = keep.tile([P, 2, H], F32, name="w1_hi", align_bytes=64)
-        w1_rows = w1.rearrange("(p j) h -> p j h", j=PACK)
-        w3w_raw = keep.tile([P, 2 * N], U8, name="w3w_raw", align_bytes=64)
+        w1_raw = w_pool.tile([P, PACK, H], F32, name="w1_raw", align_bytes=64, offset=0)
+        w3s_raw = keep.tile([P, N], U8, name="w3s_raw", align_bytes=64)
 
         def move_to_plane(plane, rows):
             for q in range(4):
-                nc.sync.dma_start(plane[32 * q : 32 * q + 4, :].bitcast(I32), rows[4 * q : 4 * q + 4, :].bitcast(I32))
+                first = ROWS_AT + 4 * q
+                nc.sync.dma_start(plane[32 * q : 32 * q + 4, :].bitcast(I32), rows[first : first + 4, :].bitcast(I32))
 
-        nc.vector.memset(xs_all[64:, :].bitcast(I32), 0)
-        nc.vector.memset(xs_all[32:64, :].bitcast(I32), 0)
+        nc.vector.memset(xs_all[:ROWS_AT, :].bitcast(I32), 0)
+        nc.vector.memset(w3s_raw[:ROWS_AT, :].bitcast(I32), 0)
         nc.vector.memset(xs[:].bitcast(I32), 0)
-        nc.sync.dma_start(xs_all[:BLOCKS, :].bitcast(I32), x_scales[0].bitcast(I32))
-        nc.scalar.dma_start(xs_all[BLOCKS : 2 * BLOCKS, :].bitcast(I32), x_scales[0].bitcast(I32))
         nc.sync.dma_start(offs_t[:], offs)
         nc.sync.dma_start(la_t[:], la)
-        nc.sync.dma_start(w3w_raw[:].bitcast(I32), w3_words[0].bitcast(I32))
-        nc.sync.dma_start(xw_all[:].bitcast(I32), x_words[0].rearrange("p c r -> p (c r)").bitcast(I32))
-        nc.sync.dma_start(w1_lo[:], w1_rows[:, :2])
-        nc.sync.dma_start(w1_hi[:], w1_rows[:, 2:])
         nc.sync.dma_start(lb_t[:], lb)
+        nc.scalar.dma_start(xs_all[ROWS_AT:, :].bitcast(I32), x_scales[0].bitcast(I32))
+        nc.scalar.dma_start(w3s_raw[ROWS_AT:, :].bitcast(I32), w3_scales[0].bitcast(I32))
+        nc.scalar.dma_start(w1_raw[:], w1.rearrange("(p j) h -> p j h", j=PACK))
+        nc.scalar.dma_start(xw_all[:].bitcast(I32), x_words[0].rearrange("p c r -> p (c r)").bitcast(I32))
 
         xs_rows = keep.tile([P, S], U8, name="xs_rows", align_bytes=64)
         nc.vector.tensor_copy(xs_rows[:], xs_all[:].indirect(offs_t[:]))
         move_to_plane(xs, xs_rows)
+        w3s_rows = keep.tile([P, N], U8, name="w3s_rows", align_bytes=64)
+        nc.vector.tensor_copy(w3s_rows[:].rearrange("p (t m) -> p t m", t=PACK), w3s_raw[:].rearrange("p (m t) -> p t m", t=PACK))
 
-        wa_t = xs_pool.tile([P, V], F32, name="wa_t", align_bytes=64, offset=0)
-        nc.sync.dma_start(wa_t[:], wa.rearrange("(p j) v -> p j v", j=PACK)[:, 0, :])
-        w3s_raw = xs_pool.tile([P, N], U8, name="w3s_raw", align_bytes=64, offset=4 * V)
-        nc.gpsimd.memset(w3s_raw[:].bitcast(I32), 0)
-        nc.sync.dma_start(w3s_raw[:BLOCKS, :].bitcast(I32), w3_scales[0].bitcast(I32))
-
-        w3w = keep.tile([P, 2 * N], U8, name="w3w", align_bytes=64)
-        nc.vector.tensor_copy(
-            w3w[:].rearrange("p (t m b) -> p t m b", t=PACK, b=2), w3w_raw[:].rearrange("p (m t b) -> p t m b", t=PACK, b=2)
-        )
-
-        xw = keep.tile([P, S], U32, name="xw", align_bytes=64)
-        nc.vector.tensor_copy(xw[:], xw_all[:].indirect(offs_t[:]))
-        w2_raw = xw_pool.tile([P, PACK, H], F32, name="w2_raw", align_bytes=64, offset=8 * V)
-        wb_t = xw_pool.tile([P, V], F32, name="wb_t", align_bytes=64, offset=4 * V)
-        nc.sync.dma_start(w2_raw[:], w2.rearrange("(p j) h -> p j h", j=PACK))
-        nc.sync.dma_start(wb_t[:], wb.rearrange("(p j) v -> p j v", j=PACK)[:, 0, :])
-
-        def deal_weights(raw, dealt, ms, ts, copy, js=slice(0, PACK)):
+        def deal_weights(raw, dealt, ms, copy):
             copy(
-                dealt[:].rearrange("p (t m j) -> p m t j", t=PACK, j=PACK)[:, ms, ts, js],
-                raw[:].rearrange("p j (m t) -> p m t j", t=PACK)[:, ms, ts],
+                dealt[:].rearrange("p (t m j) -> p m t j", t=PACK, j=PACK)[:, ms],
+                raw[:].rearrange("p j (m t) -> p m t j", t=PACK)[:, ms],
             )
 
-        w1_dealt = keep.tile([P, PACK * H], BF16, name="w1_dealt", align_bytes=64)
+        w1_dealt = d_pool.tile([P, PACK * H], BF16, name="w1_dealt", align_bytes=64, offset=0)
         w2_dealt = z_pool.tile([P, PACK * H], BF16, name="w2_dealt", align_bytes=64, offset=0)
         w1_codes = keep.tile([P, H], U32, name="w1_codes", align_bytes=64)
         w2_codes = keep.tile([P, H], U32, name="w2_codes", align_bytes=64)
         w1_sc = keep.tile([P, H], U8, name="w1_sc", align_bytes=64)
         w2_sc = keep.tile([P, H], U8, name="w2_sc", align_bytes=64)
 
-        def quantize_w1(c0, c1):
-            nc.vector.quantize_mx(w1_codes[:, c0:c1].bitcast(FP8X4), w1_sc[:, c0:c1], w1_dealt[:, PACK * c0 : PACK * c1])
+        deal_weights(w1_raw, w1_dealt, slice(0, W1_SHARE), nc.scalar.copy)
+        deal_weights(w1_raw, w1_dealt, slice(W1_SHARE, P), nc.vector.tensor_copy)
+        nc.vector.quantize_mx(w1_codes[:].bitcast(FP8X4), w1_sc[:], w1_dealt[:])
 
-        every_t, first_t, later_t = slice(0, PACK), slice(0, 1), slice(1, PACK)
-        lo_slots, hi_slots = slice(0, 2), slice(2, PACK)
-        deal_weights(w1_lo, w1_dealt, slice(0, W1_EARLY_SHARE), every_t, nc.scalar.copy, lo_slots)
-        deal_weights(w1_lo, w1_dealt, slice(W1_EARLY_SHARE, P), every_t, nc.vector.tensor_copy, lo_slots)
-        deal_weights(w1_hi, w1_dealt, slice(0, P), first_t, nc.vector.tensor_copy, hi_slots)
-        quantize_w1(0, P)
-        deal_weights(w1_hi, w1_dealt, slice(0, W1_LATE_SHARE), later_t, nc.scalar.copy, hi_slots)
-        deal_weights(w1_hi, w1_dealt, slice(W1_LATE_SHARE, P), later_t, nc.vector.tensor_copy, hi_slots)
-        quantize_w1(P, 2 * P)
-        quantize_w1(2 * P, H)
+        w3w_raw = w_pool.tile([P, 2 * N], U8, name="w3w_raw", align_bytes=64, offset=0)
+        wa_t = w_pool.tile([P, V], F32, name="wa_t", align_bytes=64, offset=2 * N)
+        w2_raw = w_pool.tile([P, PACK, H], F32, name="w2_raw", align_bytes=64, offset=2 * N + 4 * V)
+        nc.sync.dma_start(w3w_raw[:].bitcast(I32), w3_words[0].bitcast(I32))
+        nc.sync.dma_start(wa_t[:], wa.rearrange("(p j) v -> p j v", j=PACK)[:, 0, :])
+        nc.sync.dma_start(w2_raw[:], w2.rearrange("(p j) h -> p j h", j=PACK))
+
         halves = (slice(0, S // 2), slice(S // 2, S))
-        w3s_rows = keep.tile([P, N], U8, name="w3s_rows", align_bytes=64)
-        nc.vector.tensor_copy(w3s_rows[:].rearrange("p (t m) -> p t m", t=PACK), w3s_raw[:].rearrange("p (m t) -> p t m", t=PACK))
+        xw = d_pool.tile([P, S], U32, name="xw", align_bytes=64, offset=0)
+        for h, tokens in enumerate(halves):
+            nc.vector.tensor_copy(xw[:, tokens], xw_all[:].indirect(offs_t[:, 16 * h : 16 * (h + 1)]))
+        wb_t = xw_pool.tile([P, V], F32, name="wb_t", align_bytes=64, offset=0)
+        nc.sync.dma_start(wb_t[:], wb.rearrange("(p j) v -> p j v", j=PACK)[:, 0, :])
 
-        def first_layer(codes, scales, tiles, order, first_pieces):
-            for t in order:
-                cols = slice(t * P, (t + 1) * P)
-                for tokens in first_pieces if t == order[0] else (slice(0, S),):
-                    acc = psum.tile([P, tokens.stop - tokens.start], F32, name="acc", tag="acc")
-                    nc.tensor.matmul_mx(
-                        acc[:], codes[:, cols].bitcast(FP8X4), scales[:, cols], xw[:, tokens].bitcast(FP8X4), xs[:, tokens], start=True, stop=True
-                    )
-                    nc.scalar.activation(tiles[t][:, tokens], acc[:], RELU)
+        w3w = xw_pool.tile([P, 2 * N], U8, name="w3w", align_bytes=64, offset=4 * V)
+        nc.vector.tensor_copy(
+            w3w[:].rearrange("p (t m b) -> p t m b", t=PACK, b=2), w3w_raw[:].rearrange("p (m t b) -> p t m b", t=PACK, b=2)
+        )
+
+        def scalar_relu(dst, acc):
+            nc.scalar.activation(dst, acc, RELU)
+
+        def vector_relu(dst, acc):
+            nc.vector.tensor_scalar_max(dst, acc, 0.0)
+
+        def first_layer(codes, scales, tile, t, tokens, relu):
+            cols = slice(t * P, (t + 1) * P)
+            acc = psum.tile([P, tokens.stop - tokens.start], F32, name="acc", tag="acc")
+            nc.tensor.matmul_mx(
+                acc[:], codes[:, cols].bitcast(FP8X4), scales[:, cols], xw[:, tokens].bitcast(FP8X4), xs[:, tokens], start=True, stop=True
+            )
+            relu(tile[:, tokens], acc[:])
 
         relu_y = [keep.tile([P, S], F32, name="relu_y%d" % t, align_bytes=64) for t in range(PACK)]
         relu_e = [keep.tile([P, S], F32, name="relu_e%d" % t, align_bytes=64) for t in range(PACK)]
-        first_layer(w1_codes, w1_sc, relu_y, (0, 1, 2, 3), halves)
+        quarters = (slice(256, 384), slice(384, 512))
+        first_layer(w1_codes, w1_sc, relu_y[0], 0, halves[0], scalar_relu)
+        first_layer(w1_codes, w1_sc, relu_y[1], 1, halves[0], vector_relu)
+        for t in range(2):
+            for tokens in quarters:
+                first_layer(w1_codes, w1_sc, relu_y[t], t, tokens, scalar_relu)
+        for t in range(2, PACK):
+            for tokens in halves:
+                first_layer(w1_codes, w1_sc, relu_y[t], t, tokens, scalar_relu)
 
         for m0 in range(0, P, W2_STEP):
-            deal_weights(w2_raw, w2_dealt, slice(m0, m0 + W2_STEP), every_t, nc.scalar.copy)
+            deal_weights(w2_raw, w2_dealt, slice(m0, m0 + W2_STEP), nc.scalar.copy)
 
         z_bf = keep.tile([P, S, PACK], BF16, name="z_bf", align_bytes=64)
 
@@ -154,7 +154,8 @@ def tile_picked_moe2w_relu_po_kernel(
                 ahead = gather(relu_y[t + 1], la_t, wa_t)
             if t == 2:
                 nc.vector.quantize_mx(w2_codes[:].bitcast(FP8X4), w2_sc[:], w2_dealt[:])
-                first_layer(w2_codes, w2_sc, relu_e, (1, 0, 2, 3), (slice(0, S),))
+                for u in (1, 0, 2, 3):
+                    first_layer(w2_codes, w2_sc, relu_e[u], u, slice(0, S), scalar_relu)
             z.append(z_pool.tile([P, S], F32, name="z%d" % t, align_bytes=64, offset=4 * S * ((t + 2) % PACK)))
             scatter(t, picked, la_t)
             picked = ahead

@@ -58,13 +58,13 @@ def tile_picked_moe2w_relu_po_kernel(
         nc.vector.memset(xs_all[:ROWS_AT, :].bitcast(I32), 0)
         nc.vector.memset(w3s_raw[:ROWS_AT, :].bitcast(I32), 0)
         nc.vector.memset(xs[:].bitcast(I32), 0)
+        nc.scalar.dma_start(xs_all[ROWS_AT:, :].bitcast(I32), x_scales[0].bitcast(I32))
         nc.sync.dma_start(offs_t[:], offs)
+        nc.scalar.dma_start(w3s_raw[ROWS_AT:, :].bitcast(I32), w3_scales[0].bitcast(I32))
+        nc.sync.dma_start(w1_raw[:], w1.rearrange("(p j) h -> p j h", j=PACK))
         nc.sync.dma_start(la_t[:], la)
         nc.sync.dma_start(lb_t[:], lb)
-        nc.scalar.dma_start(xs_all[ROWS_AT:, :].bitcast(I32), x_scales[0].bitcast(I32))
-        nc.scalar.dma_start(w3s_raw[ROWS_AT:, :].bitcast(I32), w3_scales[0].bitcast(I32))
-        nc.scalar.dma_start(w1_raw[:], w1.rearrange("(p j) h -> p j h", j=PACK))
-        nc.scalar.dma_start(xw_all[:].bitcast(I32), x_words[0].rearrange("p c r -> p (c r)").bitcast(I32))
+        nc.sync.dma_start(xw_all[:].bitcast(I32), x_words[0].rearrange("p c r -> p (c r)").bitcast(I32))
 
         xs_rows = keep.tile([P, S], U8, name="xs_rows", align_bytes=64)
         nc.vector.tensor_copy(xs_rows[:], xs_all[:].indirect(offs_t[:]))

@@ -21,6 +21,7 @@ PACK = 4
 BLOCKS = 16
 CHUNK = 128
 ROWS_AT = P - BLOCKS
+W3_ROWS_AT = 64 - BLOCKS
 W1_SHARE = 44
 W2_STEP = 32
 WARM_PASSES = 3
@@ -50,17 +51,18 @@ def tile_picked_moe2w_relu_po_kernel(
         w1_raw = w_pool.tile([P, PACK, H], F32, name="w1_raw", align_bytes=64, offset=0)
         w3s_raw = keep.tile([P, N], U8, name="w3s_raw", align_bytes=64)
 
-        def move_to_plane(plane, rows):
+        def move_to_plane(plane, rows, rows_at):
             for q in range(4):
-                first = ROWS_AT + 4 * q
+                first = rows_at + 4 * q
                 nc.sync.dma_start(plane[32 * q : 32 * q + 4, :].bitcast(I32), rows[first : first + 4, :].bitcast(I32))
 
         nc.vector.memset(xs_all[:ROWS_AT, :].bitcast(I32), 0)
-        nc.vector.memset(w3s_raw[:ROWS_AT, :].bitcast(I32), 0)
+        nc.vector.memset(w3s_raw[:W3_ROWS_AT, :].bitcast(I32), 0)
+        nc.vector.memset(w3s_raw[64:, :].bitcast(I32), 0)
         nc.vector.memset(xs[:].bitcast(I32), 0)
         nc.scalar.dma_start(xs_all[ROWS_AT:, :].bitcast(I32), x_scales[0].bitcast(I32))
         nc.sync.dma_start(offs_t[:], offs)
-        nc.scalar.dma_start(w3s_raw[ROWS_AT:, :].bitcast(I32), w3_scales[0].bitcast(I32))
+        nc.scalar.dma_start(w3s_raw[W3_ROWS_AT:64, :].bitcast(I32), w3_scales[0].bitcast(I32))
         nc.sync.dma_start(w1_raw[:], w1.rearrange("(p j) h -> p j h", j=PACK))
         nc.sync.dma_start(la_t[:], la)
         nc.sync.dma_start(lb_t[:], lb)
@@ -68,7 +70,7 @@ def tile_picked_moe2w_relu_po_kernel(
 
         xs_rows = keep.tile([P, S], U8, name="xs_rows", align_bytes=64)
         nc.vector.tensor_copy(xs_rows[:], xs_all[:].indirect(offs_t[:]))
-        move_to_plane(xs, xs_rows)
+        move_to_plane(xs, xs_rows, ROWS_AT)
         w3s_rows = keep.tile([P, N], U8, name="w3s_rows", align_bytes=64)
         nc.vector.tensor_copy(w3s_rows[:].rearrange("p (t m) -> p t m", t=PACK), w3s_raw[:].rearrange("p (m t) -> p t m", t=PACK))
 
@@ -166,7 +168,7 @@ def tile_picked_moe2w_relu_po_kernel(
             if t == 2:
                 w3s = ring.tile([P, N], U8, name="w3s", tag="picked", align_bytes=64)
                 nc.gpsimd.memset(w3s[:].bitcast(I32), 0)
-                move_to_plane(w3s, w3s_rows)
+                move_to_plane(w3s, w3s_rows, W3_ROWS_AT)
                 warm = psum.tile([P, S], F32, name="acc", tag="acc")
                 for u in range(WARM_PASSES):
                     nc.tensor.matmul_mx(
@@ -226,8 +228,8 @@ def tile_picked_moe2w_relu_po_kernel(
         res0 = keep.tile([P, PACK, CHUNK], F32, name="res0", align_bytes=64)
         res1 = keep.tile([P, PACK, CHUNK], F32, name="res1", align_bytes=64)
         res23 = keep.tile([P, PACK, 2 * CHUNK], F32, name="res23", align_bytes=64)
-        nc.scalar.copy(res0[:, :2], acc0_lo[:])
-        nc.vector.tensor_copy(res0[:, 2:], acc0_hi[:])
+        nc.vector.tensor_copy(res0[:, :2], acc0_lo[:])
+        nc.scalar.copy(res0[:, 2:], acc0_hi[:])
         nc.sync.dma_start(out_rows[:, :, chunks[0]], res0[:])
         nc.scalar.copy(res1[:], acc1[:])
         nc.sync.dma_start(out_rows[:, :, chunks[1]], res1[:])
@@ -244,5 +246,5 @@ def tile_picked_moe2w_relu_po_kernel(
         quantize_out(chunks[3])
         store_words(chunks[3])
         for q in range(4):
-            queue = nc.scalar if q < 2 else nc.sync
+            queue = nc.scalar if q == 0 else nc.sync
             queue.dma_start(out_2[0, 4 * q : 4 * q + 4, :].bitcast(I32), o_sc[32 * q : 32 * q + 4, :].bitcast(I32))

@@ -51,26 +51,26 @@ def tile_picked_moe2w_relu_po_kernel(
         w1_raw = w_pool.tile([P, PACK, H], F32, name="w1_raw", align_bytes=64, offset=0)
         w3s_raw = keep.tile([P, N], U8, name="w3s_raw", align_bytes=64)
 
-        def move_to_plane(plane, rows, rows_at):
+        def move_to_plane(plane, rows, rows_at, count):
             for q in range(4):
                 first = rows_at + 4 * q
-                nc.sync.dma_start(plane[32 * q : 32 * q + 4, :].bitcast(I32), rows[first : first + 4, :].bitcast(I32))
+                nc.sync.dma_start(plane[32 * q : 32 * q + count, :].bitcast(I32), rows[first : first + count, :].bitcast(I32))
 
         nc.vector.memset(xs_all[:ROWS_AT, :].bitcast(I32), 0)
         nc.vector.memset(w3s_raw[:W3_ROWS_AT, :].bitcast(I32), 0)
         nc.vector.memset(w3s_raw[64:, :].bitcast(I32), 0)
         nc.vector.memset(xs[:].bitcast(I32), 0)
-        nc.scalar.dma_start(xs_all[ROWS_AT:, :].bitcast(I32), x_scales[0].bitcast(I32))
+        nc.sync.dma_start(xs_all[ROWS_AT:, :].bitcast(I32), x_scales[0].bitcast(I32))
         nc.sync.dma_start(offs_t[:], offs)
         nc.scalar.dma_start(w3s_raw[W3_ROWS_AT:64, :].bitcast(I32), w3_scales[0].bitcast(I32))
         nc.sync.dma_start(w1_raw[:], w1.rearrange("(p j) h -> p j h", j=PACK))
         nc.sync.dma_start(la_t[:], la)
-        nc.sync.dma_start(lb_t[:], lb)
         nc.sync.dma_start(xw_all[:].bitcast(I32), x_words[0].rearrange("p c r -> p (c r)").bitcast(I32))
+        nc.sync.dma_start(lb_t[:], lb)
 
         xs_rows = keep.tile([P, S], U8, name="xs_rows", align_bytes=64)
         nc.vector.tensor_copy(xs_rows[:], xs_all[:].indirect(offs_t[:]))
-        move_to_plane(xs, xs_rows, ROWS_AT)
+        move_to_plane(xs, xs_rows, ROWS_AT, 4)
         w3s_rows = keep.tile([P, N], U8, name="w3s_rows", align_bytes=64)
         nc.vector.tensor_copy(w3s_rows[:].rearrange("p (t m) -> p t m", t=PACK), w3s_raw[:].rearrange("p (m t) -> p t m", t=PACK))
 
@@ -167,8 +167,7 @@ def tile_picked_moe2w_relu_po_kernel(
                 ahead = gather(relu_e[t + 1], lb_t, wb_t)
             if t == 2:
                 w3s = ring.tile([P, N], U8, name="w3s", tag="picked", align_bytes=64)
-                nc.gpsimd.memset(w3s[:].bitcast(I32), 0)
-                move_to_plane(w3s, w3s_rows, W3_ROWS_AT)
+                move_to_plane(w3s, w3s_rows, W3_ROWS_AT, 32)
                 warm = psum.tile([P, S], F32, name="acc", tag="acc")
                 for u in range(WARM_PASSES):
                     nc.tensor.matmul_mx(

@@ -14,17 +14,16 @@ U8 = mybir.dt.uint8
 FP8X4 = mybir.dt.float8_e4m3fn_x4
 FP4X4 = mybir.dt.float4_e2m1fn_x4
 RELU = mybir.ActivationFunctionType.Relu
+COPY = mybir.ActivationFunctionType.Copy
 MULT = mybir.AluOpType.mult
 
 P = 128
 PACK = 4
 BLOCKS = 16
 CHUNK = 128
-ROWS_AT = P - BLOCKS
+X_ROWS_AT = P - BLOCKS
 W3_ROWS_AT = 64 - BLOCKS
 W1_SHARE = 44
-W2_STEP = 32
-WARM_PASSES = 3
 
 
 def tile_picked_moe2w_relu_po_kernel(
@@ -34,21 +33,22 @@ def tile_picked_moe2w_relu_po_kernel(
     with ExitStack() as ctx:
         lists = ctx.enter_context(tc.tile_pool(name="lists", bufs=1))
         keep = ctx.enter_context(tc.tile_pool(name="keep", bufs=1))
-        ring = ctx.enter_context(tc.tile_pool(name="ring", bufs=3))
         w_pool = ctx.enter_context(tc.tile_pool(name="w_pool", bufs=1))
         xw_pool = ctx.enter_context(tc.tile_pool(name="xw_pool", bufs=1))
         d_pool = ctx.enter_context(tc.tile_pool(name="d_pool", bufs=1))
-        z_pool = ctx.enter_context(tc.tile_pool(name="z_pool", bufs=1))
-        psum = ctx.enter_context(tc.psum_pool(name="psum", bufs=8))
+        e_pool = ctx.enter_context(tc.tile_pool(name="e_pool", bufs=1))
+        y_pool = ctx.enter_context(tc.tile_pool(name="y_pool", bufs=1))
+        psum = ctx.enter_context(tc.psum_pool(name="psum", bufs=7))
+        chain = ctx.enter_context(tc.psum_pool(name="chain", bufs=1))
 
         offs_t = lists.tile([P, S // 16], U16, name="offs_t")
         la_t = lists.tile([P, V // 16], U16, name="la_t")
         lb_t = lists.tile([P, V // 16], U16, name="lb_t")
 
-        xs_all = keep.tile([P, T], U8, name="xs_all", align_bytes=64)
+        xs_all = w_pool.tile([P, T], U8, name="xs_all", align_bytes=64, offset=2 * N)
         xs = keep.tile([P, S], U8, name="xs", align_bytes=64)
         xw_all = xw_pool.tile([P, T], U32, name="xw_all", align_bytes=64, offset=0)
-        w1_raw = w_pool.tile([P, PACK, H], F32, name="w1_raw", align_bytes=64, offset=0)
+        w1_raw = keep.tile([P, PACK, H], F32, name="w1_raw", align_bytes=64)
         w3s_raw = keep.tile([P, N], U8, name="w3s_raw", align_bytes=64)
 
         def move_to_plane(plane, rows, rows_at, count):
@@ -56,11 +56,11 @@ def tile_picked_moe2w_relu_po_kernel(
                 first = rows_at + 4 * q
                 nc.sync.dma_start(plane[32 * q : 32 * q + count, :].bitcast(I32), rows[first : first + count, :].bitcast(I32))
 
-        nc.vector.memset(xs_all[:ROWS_AT, :].bitcast(I32), 0)
+        nc.vector.memset(xs_all[:X_ROWS_AT, :].bitcast(I32), 0)
         nc.vector.memset(w3s_raw[:W3_ROWS_AT, :].bitcast(I32), 0)
         nc.vector.memset(w3s_raw[64:, :].bitcast(I32), 0)
         nc.vector.memset(xs[:].bitcast(I32), 0)
-        nc.sync.dma_start(xs_all[ROWS_AT:, :].bitcast(I32), x_scales[0].bitcast(I32))
+        nc.sync.dma_start(xs_all[X_ROWS_AT:, :].bitcast(I32), x_scales[0].bitcast(I32))
         nc.sync.dma_start(offs_t[:], offs)
         nc.scalar.dma_start(w3s_raw[W3_ROWS_AT:64, :].bitcast(I32), w3_scales[0].bitcast(I32))
         nc.sync.dma_start(w1_raw[:], w1.rearrange("(p j) h -> p j h", j=PACK))
@@ -70,45 +70,42 @@ def tile_picked_moe2w_relu_po_kernel(
 
         xs_rows = keep.tile([P, S], U8, name="xs_rows", align_bytes=64)
         nc.vector.tensor_copy(xs_rows[:], xs_all[:].indirect(offs_t[:]))
-        move_to_plane(xs, xs_rows, ROWS_AT, 4)
+        move_to_plane(xs, xs_rows, X_ROWS_AT, 4)
         w3s_rows = keep.tile([P, N], U8, name="w3s_rows", align_bytes=64)
         nc.vector.tensor_copy(w3s_rows[:].rearrange("p (t m) -> p t m", t=PACK), w3s_raw[:].rearrange("p (m t) -> p t m", t=PACK))
 
-        def deal_weights(raw, dealt, ms, copy):
+        def deal_weights(raw, dealt, ms, ts, copy):
             copy(
-                dealt[:].rearrange("p (t m j) -> p m t j", t=PACK, j=PACK)[:, ms],
-                raw[:].rearrange("p j (m t) -> p m t j", t=PACK)[:, ms],
+                dealt[:].rearrange("p (t m j) -> p m j t", m=P, j=PACK)[:, ms],
+                raw[:].rearrange("p j (m t) -> p m j t", t=PACK)[:, ms, :, ts],
             )
 
         w1_dealt = d_pool.tile([P, PACK * H], BF16, name="w1_dealt", align_bytes=64, offset=0)
-        w2_dealt = z_pool.tile([P, PACK * H], BF16, name="w2_dealt", align_bytes=64, offset=0)
         w1_codes = keep.tile([P, H], U32, name="w1_codes", align_bytes=64)
-        w2_codes = keep.tile([P, H], U32, name="w2_codes", align_bytes=64)
+        w2_codes = [keep.tile([P, H // 2], U32, name="w2_codes%d" % u, align_bytes=64) for u in range(2)]
         w1_sc = keep.tile([P, H], U8, name="w1_sc", align_bytes=64)
-        w2_sc = keep.tile([P, H], U8, name="w2_sc", align_bytes=64)
+        w2_sc = [keep.tile([P, H // 2], U8, name="w2_sc%d" % u, align_bytes=64) for u in range(2)]
 
-        deal_weights(w1_raw, w1_dealt, slice(0, W1_SHARE), nc.scalar.copy)
-        deal_weights(w1_raw, w1_dealt, slice(W1_SHARE, P), nc.vector.tensor_copy)
+        deal_weights(w1_raw, w1_dealt, slice(0, W1_SHARE), slice(0, PACK), nc.scalar.copy)
+        deal_weights(w1_raw, w1_dealt, slice(W1_SHARE, P), slice(0, PACK), nc.vector.tensor_copy)
         nc.vector.quantize_mx(w1_codes[:].bitcast(FP8X4), w1_sc[:], w1_dealt[:])
 
-        w3w_raw = w_pool.tile([P, 2 * N], U8, name="w3w_raw", align_bytes=64, offset=0)
-        wa_t = w_pool.tile([P, V], F32, name="wa_t", align_bytes=64, offset=2 * N)
-        w2_raw = w_pool.tile([P, PACK, H], F32, name="w2_raw", align_bytes=64, offset=2 * N + 4 * V)
-        nc.sync.dma_start(w3w_raw[:].bitcast(I32), w3_words[0].bitcast(I32))
-        nc.sync.dma_start(wa_t[:], wa.rearrange("(p j) v -> p j v", j=PACK)[:, 0, :])
+        w3w_raw = w_pool.tile([P, 2 * N], U8, name="w3w_raw", align_bytes=64, offset=64)
+        wa_t = w_pool.tile([P, V], F32, name="wa_t", align_bytes=64, offset=64 + 2 * N)
+        w2_at = 64 + 2 * N + 4 * V
+        w2_raw = w_pool.tile([P, PACK, H], F32, name="w2_raw", align_bytes=64, offset=w2_at)
         nc.sync.dma_start(w2_raw[:], w2.rearrange("(p j) h -> p j h", j=PACK))
+        nc.sync.dma_start(wa_t[:], wa.rearrange("(p j) v -> p j v", j=PACK)[:, 0, :])
+        nc.sync.dma_start(w3w_raw[:].bitcast(I32), w3_words[0].bitcast(I32))
 
         halves = (slice(0, S // 2), slice(S // 2, S))
         xw = d_pool.tile([P, S], U32, name="xw", align_bytes=64, offset=0)
-        for h, tokens in enumerate(halves):
-            nc.vector.tensor_copy(xw[:, tokens], xw_all[:].indirect(offs_t[:, 16 * h : 16 * (h + 1)]))
+        pieces = (slice(0, 256), slice(256, 384), slice(384, 512))
+        for tokens in pieces:
+            nc.vector.tensor_copy(xw[:, tokens], xw_all[:].indirect(offs_t[:, tokens.start // 16 : tokens.stop // 16]))
         wb_t = xw_pool.tile([P, V], F32, name="wb_t", align_bytes=64, offset=0)
         nc.sync.dma_start(wb_t[:], wb.rearrange("(p j) v -> p j v", j=PACK)[:, 0, :])
 
-        w3w = xw_pool.tile([P, 2 * N], U8, name="w3w", align_bytes=64, offset=4 * V)
-        nc.vector.tensor_copy(
-            w3w[:].rearrange("p (t m b) -> p t m b", t=PACK, b=2), w3w_raw[:].rearrange("p (m t b) -> p t m b", t=PACK, b=2)
-        )
 
         def scalar_relu(dst, acc):
             nc.scalar.activation(dst, acc, RELU)
@@ -116,70 +113,69 @@ def tile_picked_moe2w_relu_po_kernel(
         def vector_relu(dst, acc):
             nc.vector.tensor_scalar_max(dst, acc, 0.0)
 
-        def first_layer(codes, scales, tile, t, tokens, relu):
+        def first_layer(codes, scales, tile, t, tokens, relu, banks=psum):
             cols = slice(t * P, (t + 1) * P)
-            acc = psum.tile([P, tokens.stop - tokens.start], F32, name="acc", tag="acc")
+            acc = banks.tile([P, tokens.stop - tokens.start], F32, name="acc", tag="acc")
             nc.tensor.matmul_mx(
                 acc[:], codes[:, cols].bitcast(FP8X4), scales[:, cols], xw[:, tokens].bitcast(FP8X4), xs[:, tokens], start=True, stop=True
             )
             relu(tile[:, tokens], acc[:])
 
-        relu_y = [keep.tile([P, S], F32, name="relu_y%d" % t, align_bytes=64) for t in range(PACK)]
-        relu_e = [keep.tile([P, S], F32, name="relu_e%d" % t, align_bytes=64) for t in range(PACK)]
-        quarters = (slice(256, 384), slice(384, 512))
-        first_layer(w1_codes, w1_sc, relu_y[0], 0, halves[0], scalar_relu)
-        first_layer(w1_codes, w1_sc, relu_y[1], 1, halves[0], vector_relu)
-        for t in range(2):
-            for tokens in quarters:
-                first_layer(w1_codes, w1_sc, relu_y[t], t, tokens, scalar_relu)
-        for t in range(2, PACK):
-            for tokens in halves:
-                first_layer(w1_codes, w1_sc, relu_y[t], t, tokens, scalar_relu)
+        z = {t: keep.tile([P, S], F32, name="z%d" % t, align_bytes=64) for t in (1, 3)}
 
-        for m0 in range(0, P, W2_STEP):
-            deal_weights(w2_raw, w2_dealt, slice(m0, m0 + W2_STEP), nc.scalar.copy)
+        def look_up_and_put(name, src, idx, weight, t):
+            picked = keep.tile([P, V], F32, name=name, align_bytes=64)
+            nc.scalar.activation(picked[:], src[:].indirect(idx[:]), COPY)
+            nc.vector.tensor_tensor(z[t][:].indirect(idx[:]), picked[:], weight[:], MULT)
 
-        z_bf = keep.tile([P, S, PACK], BF16, name="z_bf", align_bytes=64)
+        def quantize_w2(pair, dealt, copy, step):
+            for m0 in range(0, P, step):
+                deal_weights(w2_raw, dealt, slice(m0, m0 + step), slice(2 * pair, 2 * pair + 2), copy)
+            nc.vector.quantize_mx(w2_codes[pair][:].bitcast(FP8X4), w2_sc[pair][:], dealt[:])
 
-        def gather(src, idx, weight):
-            picked = ring.tile([P, V], F32, name="picked", tag="picked", align_bytes=64)
-            nc.vector.tensor_tensor(picked[:], src[:].indirect(idx[:]), weight[:], MULT)
-            return picked
+        whole = slice(0, S)
+        relu_y = [
+            keep.tile([P, S], F32, name="relu_y0", align_bytes=64),
+            e_pool.tile([P, S], F32, name="relu_y1", align_bytes=64, offset=2 * S),
+            e_pool.tile([P, S], F32, name="relu_y2", align_bytes=64, offset=8 * S),
+        ]
+        first_layer(w1_codes, w1_sc, relu_y[0], 0, pieces[0], scalar_relu)
+        first_layer(w1_codes, w1_sc, relu_y[0], 0, pieces[1], scalar_relu)
+        first_layer(w1_codes, w1_sc, relu_y[0], 0, pieces[2], scalar_relu, chain)
+        first_layer(w1_codes, w1_sc, relu_y[1], 1, whole, scalar_relu, chain)
+        w2_dealt0 = xw_pool.tile([P, PACK * H // 2], BF16, name="w2_dealt0", align_bytes=64, offset=4 * V)
+        quantize_w2(0, w2_dealt0, nc.vector.tensor_copy, P)
+        z[0] = y_pool.tile([P, S], F32, name="z0", align_bytes=64, offset=0)
+        z[2] = y_pool.tile([P, S], F32, name="z2", align_bytes=64, offset=4 * S)
+        look_up_and_put("a0", relu_y[0], la_t, wa_t, 0)
+        look_up_and_put("a1", relu_y[1], la_t, wa_t, 1)
+        first_layer(w1_codes, w1_sc, relu_y[2], 2, whole, scalar_relu, chain)
+        look_up_and_put("a2", relu_y[2], la_t, wa_t, 2)
+        w2_dealt1 = e_pool.tile([P, PACK * H // 2], BF16, name="w2_dealt1", align_bytes=64, offset=0)
+        quantize_w2(1, w2_dealt1, nc.scalar.copy, P // 2)
+        for t in range(3):
+            relu_e = e_pool.tile([P, S], F32, name="relu_e%d" % t, align_bytes=64, offset=4 * S * (1 + t % 2))
+            first_layer(w2_codes[t // 2], w2_sc[t // 2], relu_e, t % 2, whole, scalar_relu)
+            look_up_and_put("b%d" % t, relu_e, lb_t, wb_t, t)
+        relu_y3 = e_pool.tile([P, S], F32, name="relu_y3", align_bytes=64, offset=8 * S)
+        w3s = w_pool.tile([P, N], U8, name="w3s", align_bytes=64, offset=w2_at)
+        move_to_plane(w3s, w3s_rows, W3_ROWS_AT, 32)
+        first_layer(w1_codes, w1_sc, relu_y3, 3, whole, scalar_relu)
+        look_up_and_put("a3", relu_y3, la_t, wa_t, 3)
+        relu_e3 = e_pool.tile([P, S], F32, name="relu_e3", align_bytes=64, offset=4 * S * 3)
+        first_layer(w2_codes[1], w2_sc[1], relu_e3, 1, whole, scalar_relu)
+        look_up_and_put("b3", relu_e3, lb_t, wb_t, 3)
+        w3w = e_pool.tile([P, 2 * N], U8, name="w3w", align_bytes=64, offset=4 * S)
+        nc.scalar.copy(
+            w3w[:].bitcast(U16).rearrange("p (t m) -> p t m", t=PACK), w3w_raw[:].bitcast(U16).rearrange("p (m t) -> p t m", t=PACK)
+        )
 
-        def scatter(t, picked, idx):
-            nc.vector.tensor_copy(z[t][:].indirect(idx[:]), picked[:])
-
-        z = []
-        picked = gather(relu_y[0], la_t, wa_t)
-        for t in range(PACK):
-            if t + 1 < PACK:
-                ahead = gather(relu_y[t + 1], la_t, wa_t)
-            if t == 2:
-                nc.vector.quantize_mx(w2_codes[:].bitcast(FP8X4), w2_sc[:], w2_dealt[:])
-                for u in (1, 0, 2, 3):
-                    first_layer(w2_codes, w2_sc, relu_e[u], u, slice(0, S), scalar_relu)
-            z.append(z_pool.tile([P, S], F32, name="z%d" % t, align_bytes=64, offset=4 * S * ((t + 2) % PACK)))
-            scatter(t, picked, la_t)
-            picked = ahead
-        picked = gather(relu_e[0], lb_t, wb_t)
-        for t in range(PACK):
-            if t + 1 < PACK:
-                ahead = gather(relu_e[t + 1], lb_t, wb_t)
-            if t == 2:
-                w3s = ring.tile([P, N], U8, name="w3s", tag="picked", align_bytes=64)
-                move_to_plane(w3s, w3s_rows, W3_ROWS_AT, 32)
-                warm = psum.tile([P, S], F32, name="acc", tag="acc")
-                for u in range(WARM_PASSES):
-                    nc.tensor.matmul_mx(
-                        warm[:], w3w[:, : 2 * P].bitcast(FP4X4), w3s[:, :P], xw[:].bitcast(FP8X4), xs[:], start=True, stop=True
-                    )
-            scatter(t, picked, lb_t)
-            picked = ahead
-            if t < 2:
-                nc.scalar.copy(z_bf[:, :, t], z[t][:])
-            if t == 2:
-                nc.scalar.copy(z_bf[:, : S // 2, 2:4], z[t][:, : S // 2].unsqueeze(2).to_broadcast([P, S // 2, 2]))
-                nc.scalar.copy(z_bf[:, S // 2 :, t], z[t][:, S // 2 :])
+        z_rows = e_pool.tile([P, 3, S], BF16, name="z_rows", align_bytes=64, offset=4 * S * 3)
+        for t in range(3):
+            nc.scalar.copy(z_rows[:, t, :], z[t][:])
+        z_bf = y_pool.tile([P, S, PACK], BF16, name="z_bf", align_bytes=64, offset=4 * S)
+        nc.scalar.copy(z_bf[:, halves[0], 0:2], z_rows[:, 0:2, halves[0]].rearrange("p t s -> p s t"))
+        nc.scalar.copy(z_bf[:, halves[1], 0:3], z_rows[:, 0:3, halves[1]].rearrange("p t s -> p s t"))
 
         z_codes = keep.tile([P, S], U32, name="z_codes", align_bytes=64)
         z_sc = keep.tile([P, S], U8, name="z_sc", align_bytes=64)
@@ -189,9 +185,12 @@ def tile_picked_moe2w_relu_po_kernel(
         out_words = out_1[0].rearrange("p c r -> p (c r)").bitcast(I32)
         chunks = [slice(c, c + CHUNK) for c in range(0, S, CHUNK)]
         for c, cols in enumerate(chunks):
-            copy = nc.vector.tensor_copy if c < 2 else nc.scalar.copy
-            copy(z_bf[:, cols, PACK - 1], z[PACK - 1][:, cols])
-        for cols in chunks:
+            if c < 2:
+                nc.vector.tensor_copy(z_bf[:, cols, 2], z_rows[:, 2, cols])
+                nc.vector.tensor_copy(z_bf[:, cols, 3], z[3][:, cols])
+            else:
+                nc.scalar.copy(z_bf[:, cols, 3], z[3][:, cols])
+        for c, cols in enumerate(chunks):
             nc.vector.quantize_mx(z_codes[:, cols].bitcast(FP8X4), z_sc[:, cols], z_bf[:, cols, :].rearrange("p s t -> p (s t)"))
         res_bf = keep.tile([P, S, PACK], BF16, name="res_bf", align_bytes=64)
 

@@ -20,9 +20,12 @@ MULT = mybir.AluOpType.mult
 P = 128
 PACK = 4
 BLOCKS = 16
+QUADRANT = 32
 CHUNK = 128
+ALIGN = 64
+ROW = 4 * S
 X_ROWS_AT = P - BLOCKS
-W3_ROWS_AT = 64 - BLOCKS
+W3_ROWS_AT = P // 2 - BLOCKS
 W1_SHARE = 44
 
 
@@ -38,6 +41,7 @@ def tile_picked_moe2w_relu_po_kernel(
         d_pool = ctx.enter_context(tc.tile_pool(name="d_pool", bufs=1))
         e_pool = ctx.enter_context(tc.tile_pool(name="e_pool", bufs=1))
         y_pool = ctx.enter_context(tc.tile_pool(name="y_pool", bufs=1))
+        z_pool = ctx.enter_context(tc.tile_pool(name="z_pool", bufs=1))
         psum = ctx.enter_context(tc.psum_pool(name="psum", bufs=7))
         chain = ctx.enter_context(tc.psum_pool(name="chain", bufs=1))
 
@@ -45,33 +49,33 @@ def tile_picked_moe2w_relu_po_kernel(
         la_t = lists.tile([P, V // 16], U16, name="la_t")
         lb_t = lists.tile([P, V // 16], U16, name="lb_t")
 
-        xs_all = w_pool.tile([P, T], U8, name="xs_all", align_bytes=64, offset=2 * N)
-        xs = keep.tile([P, S], U8, name="xs", align_bytes=64)
-        xw_all = xw_pool.tile([P, T], U32, name="xw_all", align_bytes=64, offset=0)
-        w1_raw = keep.tile([P, PACK, H], F32, name="w1_raw", align_bytes=64)
-        w3s_raw = keep.tile([P, N], U8, name="w3s_raw", align_bytes=64)
+        xs_all = w_pool.tile([P, T], U8, name="xs_all", align_bytes=ALIGN, offset=2 * N)
+        xs = keep.tile([P, S], U8, name="xs", align_bytes=ALIGN)
+        xw_all = xw_pool.tile([P, T], U32, name="xw_all", align_bytes=ALIGN, offset=0)
+        w1_raw = keep.tile([P, PACK, H], F32, name="w1_raw", align_bytes=ALIGN)
+        w3s_raw = keep.tile([P, N], U8, name="w3s_raw", align_bytes=ALIGN)
 
         def move_to_plane(plane, rows, rows_at, count):
             for q in range(4):
                 first = rows_at + 4 * q
-                nc.sync.dma_start(plane[32 * q : 32 * q + count, :].bitcast(I32), rows[first : first + count, :].bitcast(I32))
+                nc.sync.dma_start(plane[QUADRANT * q : QUADRANT * q + count, :].bitcast(I32), rows[first : first + count, :].bitcast(I32))
 
         nc.vector.memset(xs_all[:X_ROWS_AT, :].bitcast(I32), 0)
         nc.vector.memset(w3s_raw[:W3_ROWS_AT, :].bitcast(I32), 0)
-        nc.vector.memset(w3s_raw[64:, :].bitcast(I32), 0)
+        nc.vector.memset(w3s_raw[P // 2 :, :].bitcast(I32), 0)
         nc.vector.memset(xs[:].bitcast(I32), 0)
         nc.sync.dma_start(xs_all[X_ROWS_AT:, :].bitcast(I32), x_scales[0].bitcast(I32))
         nc.sync.dma_start(offs_t[:], offs)
-        nc.scalar.dma_start(w3s_raw[W3_ROWS_AT:64, :].bitcast(I32), w3_scales[0].bitcast(I32))
+        nc.scalar.dma_start(w3s_raw[W3_ROWS_AT : P // 2, :].bitcast(I32), w3_scales[0].bitcast(I32))
         nc.sync.dma_start(w1_raw[:], w1.rearrange("(p j) h -> p j h", j=PACK))
-        nc.sync.dma_start(la_t[:], la)
         nc.sync.dma_start(xw_all[:].bitcast(I32), x_words[0].rearrange("p c r -> p (c r)").bitcast(I32))
+        nc.sync.dma_start(la_t[:], la)
         nc.sync.dma_start(lb_t[:], lb)
 
-        xs_rows = keep.tile([P, S], U8, name="xs_rows", align_bytes=64)
+        xs_rows = keep.tile([P, S], U8, name="xs_rows", align_bytes=ALIGN)
         nc.vector.tensor_copy(xs_rows[:], xs_all[:].indirect(offs_t[:]))
         move_to_plane(xs, xs_rows, X_ROWS_AT, 4)
-        w3s_rows = keep.tile([P, N], U8, name="w3s_rows", align_bytes=64)
+        w3s_rows = keep.tile([P, N], U8, name="w3s_rows", align_bytes=ALIGN)
         nc.vector.tensor_copy(w3s_rows[:].rearrange("p (t m) -> p t m", t=PACK), w3s_raw[:].rearrange("p (m t) -> p t m", t=PACK))
 
         def deal_weights(raw, dealt, ms, ts, copy):
@@ -80,32 +84,30 @@ def tile_picked_moe2w_relu_po_kernel(
                 raw[:].rearrange("p j (m t) -> p m j t", t=PACK)[:, ms, :, ts],
             )
 
-        w1_dealt = d_pool.tile([P, PACK * H], BF16, name="w1_dealt", align_bytes=64, offset=0)
-        w1_codes = keep.tile([P, H], U32, name="w1_codes", align_bytes=64)
-        w2_codes = [keep.tile([P, H // 2], U32, name="w2_codes%d" % u, align_bytes=64) for u in range(2)]
-        w1_sc = keep.tile([P, H], U8, name="w1_sc", align_bytes=64)
-        w2_sc = [keep.tile([P, H // 2], U8, name="w2_sc%d" % u, align_bytes=64) for u in range(2)]
+        w1_dealt = d_pool.tile([P, PACK * H], BF16, name="w1_dealt", align_bytes=ALIGN, offset=0)
+        w1_codes = keep.tile([P, H], U32, name="w1_codes", align_bytes=ALIGN)
+        w1_sc = keep.tile([P, H], U8, name="w1_sc", align_bytes=ALIGN)
+        w2_sc = [keep.tile([P, H // 2], U8, name="w2_sc%d" % u, align_bytes=ALIGN) for u in range(2)]
 
         deal_weights(w1_raw, w1_dealt, slice(0, W1_SHARE), slice(0, PACK), nc.scalar.copy)
         deal_weights(w1_raw, w1_dealt, slice(W1_SHARE, P), slice(0, PACK), nc.vector.tensor_copy)
         nc.vector.quantize_mx(w1_codes[:].bitcast(FP8X4), w1_sc[:], w1_dealt[:])
 
-        w3w_raw = w_pool.tile([P, 2 * N], U8, name="w3w_raw", align_bytes=64, offset=64)
-        wa_t = w_pool.tile([P, V], F32, name="wa_t", align_bytes=64, offset=64 + 2 * N)
-        w2_at = 64 + 2 * N + 4 * V
-        w2_raw = w_pool.tile([P, PACK, H], F32, name="w2_raw", align_bytes=64, offset=w2_at)
+        w3w_raw = w_pool.tile([P, 2 * N], U8, name="w3w_raw", align_bytes=ALIGN, offset=ALIGN)
+        wa_t = w_pool.tile([P, V], F32, name="wa_t", align_bytes=ALIGN, offset=ALIGN + 2 * N)
+        w2_at = ALIGN + 2 * N + 4 * V
+        w2_raw = w_pool.tile([P, PACK, H], F32, name="w2_raw", align_bytes=ALIGN, offset=w2_at)
         nc.sync.dma_start(w2_raw[:], w2.rearrange("(p j) h -> p j h", j=PACK))
         nc.sync.dma_start(wa_t[:], wa.rearrange("(p j) v -> p j v", j=PACK)[:, 0, :])
         nc.sync.dma_start(w3w_raw[:].bitcast(I32), w3_words[0].bitcast(I32))
 
         halves = (slice(0, S // 2), slice(S // 2, S))
-        xw = d_pool.tile([P, S], U32, name="xw", align_bytes=64, offset=0)
+        xw = d_pool.tile([P, S], U32, name="xw", align_bytes=ALIGN, offset=0)
         pieces = (slice(0, 256), slice(256, 384), slice(384, 512))
         for tokens in pieces:
             nc.vector.tensor_copy(xw[:, tokens], xw_all[:].indirect(offs_t[:, tokens.start // 16 : tokens.stop // 16]))
-        wb_t = xw_pool.tile([P, V], F32, name="wb_t", align_bytes=64, offset=0)
+        wb_t = xw_pool.tile([P, V], F32, name="wb_t", align_bytes=ALIGN, offset=0)
         nc.sync.dma_start(wb_t[:], wb.rearrange("(p j) v -> p j v", j=PACK)[:, 0, :])
-
 
         def scalar_relu(dst, acc):
             nc.scalar.activation(dst, acc, RELU)
@@ -113,86 +115,85 @@ def tile_picked_moe2w_relu_po_kernel(
         def vector_relu(dst, acc):
             nc.vector.tensor_scalar_max(dst, acc, 0.0)
 
-        def first_layer(codes, scales, tile, t, tokens, relu, banks=psum):
-            cols = slice(t * P, (t + 1) * P)
+        def first_layer(codes, scales, index, dst, tokens=slice(0, S), relu=scalar_relu, banks=psum):
+            cols = slice(index * P, (index + 1) * P)
             acc = banks.tile([P, tokens.stop - tokens.start], F32, name="acc", tag="acc")
             nc.tensor.matmul_mx(
                 acc[:], codes[:, cols].bitcast(FP8X4), scales[:, cols], xw[:, tokens].bitcast(FP8X4), xs[:, tokens], start=True, stop=True
             )
-            relu(tile[:, tokens], acc[:])
+            relu(dst[:, tokens], acc[:])
 
-        z = {t: keep.tile([P, S], F32, name="z%d" % t, align_bytes=64) for t in (1, 3)}
+        z = [keep.tile([P, S], F32, name="z%d" % t, align_bytes=ALIGN) for t in range(2)]
+        z.append(z_pool.tile([P, S], F32, name="z2", align_bytes=ALIGN, offset=0))
+        z.append(keep.tile([P, S], F32, name="z3", align_bytes=ALIGN))
 
         def look_up_and_put(name, src, idx, weight, t):
-            picked = keep.tile([P, V], F32, name=name, align_bytes=64)
+            picked = keep.tile([P, V], F32, name=name, align_bytes=ALIGN)
             nc.scalar.activation(picked[:], src[:].indirect(idx[:]), COPY)
             nc.vector.tensor_tensor(z[t][:].indirect(idx[:]), picked[:], weight[:], MULT)
 
-        def quantize_w2(pair, dealt, copy, step):
-            for m0 in range(0, P, step):
-                deal_weights(w2_raw, dealt, slice(m0, m0 + step), slice(2 * pair, 2 * pair + 2), copy)
-            nc.vector.quantize_mx(w2_codes[pair][:].bitcast(FP8X4), w2_sc[pair][:], dealt[:])
-
-        whole = slice(0, S)
-        relu_y = [
-            keep.tile([P, S], F32, name="relu_y0", align_bytes=64),
-            e_pool.tile([P, S], F32, name="relu_y1", align_bytes=64, offset=2 * S),
-            e_pool.tile([P, S], F32, name="relu_y2", align_bytes=64, offset=8 * S),
+        relu_y0 = y_pool.tile([P, S], F32, name="relu_y0", align_bytes=ALIGN, offset=0)
+        first_layer(w1_codes, w1_sc, 0, relu_y0, pieces[0])
+        first_layer(w1_codes, w1_sc, 0, relu_y0, pieces[1])
+        first_layer(w1_codes, w1_sc, 0, relu_y0, pieces[2], vector_relu, chain)
+        w2_dealt0 = xw_pool.tile([P, PACK * H // 2], BF16, name="w2_dealt0", align_bytes=ALIGN, offset=4 * V)
+        deal_weights(w2_raw, w2_dealt0, slice(0, P), slice(0, 2), nc.vector.tensor_copy)
+        look_up_and_put("a0", relu_y0, la_t, wa_t, 0)
+        w2_codes = [
+            y_pool.tile([P, H // 2], U32, name="w2_codes0", align_bytes=ALIGN, offset=0),
+            keep.tile([P, H // 2], U32, name="w2_codes1", align_bytes=ALIGN),
         ]
-        first_layer(w1_codes, w1_sc, relu_y[0], 0, pieces[0], scalar_relu)
-        first_layer(w1_codes, w1_sc, relu_y[0], 0, pieces[1], scalar_relu)
-        first_layer(w1_codes, w1_sc, relu_y[0], 0, pieces[2], scalar_relu, chain)
-        first_layer(w1_codes, w1_sc, relu_y[1], 1, whole, scalar_relu, chain)
-        w2_dealt0 = xw_pool.tile([P, PACK * H // 2], BF16, name="w2_dealt0", align_bytes=64, offset=4 * V)
-        quantize_w2(0, w2_dealt0, nc.vector.tensor_copy, P)
-        z[0] = y_pool.tile([P, S], F32, name="z0", align_bytes=64, offset=0)
-        z[2] = y_pool.tile([P, S], F32, name="z2", align_bytes=64, offset=4 * S)
-        look_up_and_put("a0", relu_y[0], la_t, wa_t, 0)
-        look_up_and_put("a1", relu_y[1], la_t, wa_t, 1)
-        first_layer(w1_codes, w1_sc, relu_y[2], 2, whole, scalar_relu, chain)
-        look_up_and_put("a2", relu_y[2], la_t, wa_t, 2)
-        w2_dealt1 = e_pool.tile([P, PACK * H // 2], BF16, name="w2_dealt1", align_bytes=64, offset=0)
-        quantize_w2(1, w2_dealt1, nc.scalar.copy, P // 2)
-        for t in range(3):
-            relu_e = e_pool.tile([P, S], F32, name="relu_e%d" % t, align_bytes=64, offset=4 * S * (1 + t % 2))
-            first_layer(w2_codes[t // 2], w2_sc[t // 2], relu_e, t % 2, whole, scalar_relu)
-            look_up_and_put("b%d" % t, relu_e, lb_t, wb_t, t)
-        relu_y3 = e_pool.tile([P, S], F32, name="relu_y3", align_bytes=64, offset=8 * S)
-        w3s = w_pool.tile([P, N], U8, name="w3s", align_bytes=64, offset=w2_at)
-        move_to_plane(w3s, w3s_rows, W3_ROWS_AT, 32)
-        first_layer(w1_codes, w1_sc, relu_y3, 3, whole, scalar_relu)
+        nc.vector.quantize_mx(w2_codes[0][:].bitcast(FP8X4), w2_sc[0][:], w2_dealt0[:])
+        relu_y1 = e_pool.tile([P, S], F32, name="relu_y1", align_bytes=ALIGN, offset=0)
+        relu_y2 = y_pool.tile([P, S], F32, name="relu_y2", align_bytes=ALIGN, offset=ROW // 2)
+        first_layer(w1_codes, w1_sc, 1, relu_y1, banks=chain)
+        first_layer(w1_codes, w1_sc, 2, relu_y2)
+        look_up_and_put("a1", relu_y1, la_t, wa_t, 1)
+        look_up_and_put("a2", relu_y2, la_t, wa_t, 2)
+        w2_dealt1 = e_pool.tile([P, PACK * H // 2], BF16, name="w2_dealt1", align_bytes=ALIGN, offset=0)
+        relu_e = [e_pool.tile([P, S], F32, name="relu_e%d" % t, align_bytes=ALIGN, offset=ROW * (1 + t)) for t in range(PACK)]
+        deal_weights(w2_raw, w2_dealt1, slice(0, P // 2), slice(2, 4), nc.scalar.copy)
+        first_layer(w2_codes[0], w2_sc[0], 0, relu_e[0])
+        deal_weights(w2_raw, w2_dealt1, slice(P // 2, P), slice(2, 4), nc.scalar.copy)
+        nc.vector.quantize_mx(w2_codes[1][:].bitcast(FP8X4), w2_sc[1][:], w2_dealt1[:])
+        look_up_and_put("b0", relu_e[0], lb_t, wb_t, 0)
+        w3s = w_pool.tile([P, N], U8, name="w3s", align_bytes=ALIGN, offset=w2_at)
+        move_to_plane(w3s, w3s_rows, W3_ROWS_AT, QUADRANT)
+        first_layer(w2_codes[0], w2_sc[0], 1, relu_e[1])
+        relu_y3 = e_pool.tile([P, S], F32, name="relu_y3", align_bytes=ALIGN, offset=ROW)
+        first_layer(w1_codes, w1_sc, 3, relu_y3)
+        look_up_and_put("b1", relu_e[1], lb_t, wb_t, 1)
         look_up_and_put("a3", relu_y3, la_t, wa_t, 3)
-        relu_e3 = e_pool.tile([P, S], F32, name="relu_e3", align_bytes=64, offset=4 * S * 3)
-        first_layer(w2_codes[1], w2_sc[1], relu_e3, 1, whole, scalar_relu)
-        look_up_and_put("b3", relu_e3, lb_t, wb_t, 3)
-        w3w = e_pool.tile([P, 2 * N], U8, name="w3w", align_bytes=64, offset=4 * S)
+        first_layer(w2_codes[1], w2_sc[1], 0, relu_e[2])
+        first_layer(w2_codes[1], w2_sc[1], 1, relu_e[3])
+        look_up_and_put("b2", relu_e[2], lb_t, wb_t, 2)
+        look_up_and_put("b3", relu_e[3], lb_t, wb_t, 3)
+        w3w = e_pool.tile([P, 2 * N], U8, name="w3w", align_bytes=ALIGN, offset=2 * ROW)
         nc.scalar.copy(
             w3w[:].bitcast(U16).rearrange("p (t m) -> p t m", t=PACK), w3w_raw[:].bitcast(U16).rearrange("p (m t) -> p t m", t=PACK)
         )
 
-        z_rows = e_pool.tile([P, 3, S], BF16, name="z_rows", align_bytes=64, offset=4 * S * 3)
-        for t in range(3):
+        z_rows = e_pool.tile([P, PACK - 1, S], BF16, name="z_rows", align_bytes=ALIGN, offset=4 * ROW)
+        for t in range(PACK - 1):
             nc.scalar.copy(z_rows[:, t, :], z[t][:])
-        z_bf = y_pool.tile([P, S, PACK], BF16, name="z_bf", align_bytes=64, offset=4 * S)
-        nc.scalar.copy(z_bf[:, halves[0], 0:2], z_rows[:, 0:2, halves[0]].rearrange("p t s -> p s t"))
-        nc.scalar.copy(z_bf[:, halves[1], 0:3], z_rows[:, 0:3, halves[1]].rearrange("p t s -> p s t"))
+        z_bf = z_pool.tile([P, S, PACK], BF16, name="z_bf", align_bytes=ALIGN, offset=0)
+        nc.scalar.copy(z_bf[:, halves[1], 0:3], z_rows[:, :, halves[1]].rearrange("p t s -> p s t"))
 
-        z_codes = keep.tile([P, S], U32, name="z_codes", align_bytes=64)
-        z_sc = keep.tile([P, S], U8, name="z_sc", align_bytes=64)
-        o_codes = keep.tile([P, S], U32, name="o_codes", align_bytes=64)
-        o_sc = keep.tile([P, S], U8, name="o_sc", align_bytes=64)
+        z_codes = keep.tile([P, S], U32, name="z_codes", align_bytes=ALIGN)
+        z_sc = keep.tile([P, S], U8, name="z_sc", align_bytes=ALIGN)
+        o_codes = keep.tile([P, S], U32, name="o_codes", align_bytes=ALIGN)
+        o_sc = keep.tile([P, S], U8, name="o_sc", align_bytes=ALIGN)
         out_rows = out_0.rearrange("(p t) s -> p t s", t=PACK)
         out_words = out_1[0].rearrange("p c r -> p (c r)").bitcast(I32)
         chunks = [slice(c, c + CHUNK) for c in range(0, S, CHUNK)]
-        for c, cols in enumerate(chunks):
-            if c < 2:
-                nc.vector.tensor_copy(z_bf[:, cols, 2], z_rows[:, 2, cols])
+        for cols in chunks:
+            if cols.stop <= halves[0].stop:
+                nc.vector.tensor_copy(z_bf[:, cols, 0:3], z_rows[:, :, cols].rearrange("p t s -> p s t"))
                 nc.vector.tensor_copy(z_bf[:, cols, 3], z[3][:, cols])
             else:
                 nc.scalar.copy(z_bf[:, cols, 3], z[3][:, cols])
-        for c, cols in enumerate(chunks):
             nc.vector.quantize_mx(z_codes[:, cols].bitcast(FP8X4), z_sc[:, cols], z_bf[:, cols, :].rearrange("p s t -> p (s t)"))
-        res_bf = keep.tile([P, S, PACK], BF16, name="res_bf", align_bytes=64)
+        res_bf = keep.tile([P, S, PACK], BF16, name="res_bf", align_bytes=ALIGN)
 
         def second_layer(cols, tiles):
             acc = psum.tile([P, len(tiles), CHUNK], F32, name="acc", tag="acc")
@@ -210,12 +211,12 @@ def tile_picked_moe2w_relu_po_kernel(
 
         acc0_lo = second_layer(chunks[0], (0, 1))
         acc0_hi = second_layer(chunks[0], (2, 3))
-        acc1, acc2, acc3 = [second_layer(cols, range(PACK)) for cols in chunks[1:]]
+        acc1, acc2 = [second_layer(cols, range(PACK)) for cols in chunks[1:3]]
+        acc3_lo = second_layer(chunks[3], (0, 1))
+        acc3_hi = second_layer(chunks[3], (2, 3))
 
-        def interleave(cols, res):
-            nc.vector.tensor_copy(
-                res_bf[:, cols, :].rearrange("p (s i) t -> p s t i", i=4), res.rearrange("p t (s i) -> p s t i", i=4)
-            )
+        def interleave(cols, res, copy):
+            copy(res_bf[:, cols, :].rearrange("p (s i) t -> p s t i", i=4), res.rearrange("p t (s i) -> p s t i", i=4))
 
         def quantize_out(cols):
             nc.vector.quantize_mx(o_codes[:, cols].bitcast(FP8X4), o_sc[:, cols], res_bf[:, cols, :].rearrange("p s t -> p (s t)"))
@@ -223,26 +224,26 @@ def tile_picked_moe2w_relu_po_kernel(
         def store_words(cols):
             nc.sync.dma_start(out_words[:, cols], o_codes[:, cols].bitcast(I32))
 
-        res0 = keep.tile([P, PACK, CHUNK], F32, name="res0", align_bytes=64)
-        res1 = keep.tile([P, PACK, CHUNK], F32, name="res1", align_bytes=64)
-        res23 = keep.tile([P, PACK, 2 * CHUNK], F32, name="res23", align_bytes=64)
-        nc.vector.tensor_copy(res0[:, :2], acc0_lo[:])
-        nc.scalar.copy(res0[:, 2:], acc0_hi[:])
-        nc.sync.dma_start(out_rows[:, :, chunks[0]], res0[:])
-        nc.scalar.copy(res1[:], acc1[:])
-        nc.sync.dma_start(out_rows[:, :, chunks[1]], res1[:])
-        nc.vector.tensor_copy(res23[:, :, :CHUNK], acc2[:])
-        nc.scalar.copy(res23[:, :, CHUNK:], acc3[:])
-        nc.sync.dma_start(out_rows[:, :, halves[1]], res23[:])
-        nc.scalar.copy(res_bf[:, chunks[3], :], acc3[:].rearrange("p t s -> p s t"))
-        interleave(chunks[0], res0[:])
-        interleave(chunks[1], res1[:])
-        interleave(chunks[2], res23[:, :, :CHUNK])
+        res = [keep.tile([P, PACK, CHUNK], F32, name="res%d" % c, align_bytes=ALIGN) for c in range(len(chunks))]
+        nc.vector.tensor_copy(res[0][:, :2], acc0_lo[:])
+        nc.scalar.copy(res[0][:, 2:], acc0_hi[:])
+        nc.sync.dma_start(out_rows[:, :, chunks[0]], res[0][:])
+        nc.scalar.copy(res[1][:], acc1[:])
+        nc.sync.dma_start(out_rows[:, :, chunks[1]], res[1][:])
+        nc.scalar.copy(res[2][:], acc2[:])
+        nc.sync.dma_start(out_rows[:, :, chunks[2]], res[2][:])
+        nc.vector.tensor_copy(res[3][:, :2], acc3_lo[:])
+        nc.scalar.copy(res[3][:, 2:], acc3_hi[:])
+        nc.sync.dma_start(out_rows[:, :, chunks[3]], res[3][:])
+        interleave(chunks[0], res[0][:], nc.vector.tensor_copy)
+        interleave(chunks[1], res[1][:], nc.vector.tensor_copy)
         quantize_out(halves[0])
+        interleave(chunks[2], res[2][:], nc.scalar.copy)
+        interleave(chunks[3], res[3][:], nc.vector.tensor_copy)
         quantize_out(chunks[2])
-        store_words(slice(0, 3 * CHUNK))
+        store_words(slice(0, chunks[2].stop))
         quantize_out(chunks[3])
         store_words(chunks[3])
         for q in range(4):
             queue = nc.scalar if q == 0 else nc.sync
-            queue.dma_start(out_2[0, 4 * q : 4 * q + 4, :].bitcast(I32), o_sc[32 * q : 32 * q + 4, :].bitcast(I32))
+            queue.dma_start(out_2[0, 4 * q : 4 * q + 4, :].bitcast(I32), o_sc[QUADRANT * q : QUADRANT * q + 4, :].bitcast(I32))

@@ -157,8 +157,6 @@ def tile_picked_moe2w_relu_po_kernel(
         deal_weights(w2_raw, w2_dealt1, slice(P // 2, P), slice(2, 4), nc.scalar.copy)
         nc.vector.quantize_mx(w2_codes[1][:].bitcast(FP8X4), w2_sc[1][:], w2_dealt1[:])
         look_up_and_put("b0", relu_e[0], lb_t, wb_t, 0)
-        w3s = w_pool.tile([P, N], U8, name="w3s", align_bytes=ALIGN, offset=w2_at)
-        move_to_plane(w3s, w3s_rows, W3_ROWS_AT, QUADRANT)
         first_layer(w2_codes[0], w2_sc[0], 1, relu_e[1])
         relu_y3 = e_pool.tile([P, S], F32, name="relu_y3", align_bytes=ALIGN, offset=ROW)
         first_layer(w1_codes, w1_sc, 3, relu_y3)
@@ -168,12 +166,19 @@ def tile_picked_moe2w_relu_po_kernel(
         first_layer(w2_codes[1], w2_sc[1], 1, relu_e[3])
         look_up_and_put("b2", relu_e[2], lb_t, wb_t, 2)
         look_up_and_put("b3", relu_e[3], lb_t, wb_t, 3)
+        w3s = e_pool.tile([P, N], U8, name="w3s", align_bytes=ALIGN, offset=4 * ROW)
+        move_to_plane(w3s, w3s_rows, W3_ROWS_AT, QUADRANT)
+        warm = chain.tile([32, S], F32, name="acc", tag="acc")
+        for i in range(4):
+            nc.tensor.matmul_mx(
+                warm[:], w1_codes[:, :32].bitcast(FP8X4), w3s[:, :32], w1_codes[:].bitcast(FP8X4), w1_sc[:], start=True, stop=True
+            )
         w3w = e_pool.tile([P, 2 * N], U8, name="w3w", align_bytes=ALIGN, offset=2 * ROW)
         nc.scalar.copy(
             w3w[:].bitcast(U16).rearrange("p (t m) -> p t m", t=PACK), w3w_raw[:].bitcast(U16).rearrange("p (m t) -> p t m", t=PACK)
         )
 
-        z_rows = e_pool.tile([P, PACK - 1, S], BF16, name="z_rows", align_bytes=ALIGN, offset=4 * ROW)
+        z_rows = e_pool.tile([P, PACK - 1, S], BF16, name="z_rows", align_bytes=ALIGN, offset=4 * ROW + N)
         for t in range(PACK - 1):
             nc.scalar.copy(z_rows[:, t, :], z[t][:])
         z_bf = z_pool.tile([P, S, PACK], BF16, name="z_bf", align_bytes=ALIGN, offset=0)

@@ -166,19 +166,19 @@ def tile_picked_moe2w_relu_po_kernel(
         first_layer(w2_codes[1], w2_sc[1], 1, relu_e[3])
         look_up_and_put("b2", relu_e[2], lb_t, wb_t, 2)
         look_up_and_put("b3", relu_e[3], lb_t, wb_t, 3)
-        w3s = e_pool.tile([P, N], U8, name="w3s", align_bytes=ALIGN, offset=4 * ROW)
+        w3w = e_pool.tile([P, 2 * N], U8, name="w3w", align_bytes=ALIGN, offset=2 * ROW)
+        nc.scalar.copy(
+            w3w[:].bitcast(U16).rearrange("p (t m) -> p t m", t=PACK), w3w_raw[:].bitcast(U16).rearrange("p (m t) -> p t m", t=PACK)
+        )
+
+        w3s = w_pool.tile([P, N], U8, name="w3s", align_bytes=ALIGN, offset=ALIGN)
         move_to_plane(w3s, w3s_rows, W3_ROWS_AT, QUADRANT)
         warm = chain.tile([32, S], F32, name="acc", tag="acc")
         for i in range(4):
             nc.tensor.matmul_mx(
                 warm[:], w1_codes[:, :32].bitcast(FP8X4), w3s[:, :32], w1_codes[:].bitcast(FP8X4), w1_sc[:], start=True, stop=True
             )
-        w3w = e_pool.tile([P, 2 * N], U8, name="w3w", align_bytes=ALIGN, offset=2 * ROW)
-        nc.scalar.copy(
-            w3w[:].bitcast(U16).rearrange("p (t m) -> p t m", t=PACK), w3w_raw[:].bitcast(U16).rearrange("p (m t) -> p t m", t=PACK)
-        )
-
-        z_rows = e_pool.tile([P, PACK - 1, S], BF16, name="z_rows", align_bytes=ALIGN, offset=4 * ROW + N)
+        z_rows = e_pool.tile([P, PACK - 1, S], BF16, name="z_rows", align_bytes=ALIGN, offset=4 * ROW)
         for t in range(PACK - 1):
             nc.scalar.copy(z_rows[:, t, :], z[t][:])
         z_bf = z_pool.tile([P, S, PACK], BF16, name="z_bf", align_bytes=ALIGN, offset=0)
@@ -243,7 +243,7 @@ def tile_picked_moe2w_relu_po_kernel(
         interleave(chunks[0], res[0][:], nc.vector.tensor_copy)
         interleave(chunks[1], res[1][:], nc.vector.tensor_copy)
         quantize_out(halves[0])
-        interleave(chunks[2], res[2][:], nc.scalar.copy)
+        interleave(chunks[2], acc2[:], nc.scalar.copy)
         interleave(chunks[3], res[3][:], nc.vector.tensor_copy)
         quantize_out(chunks[2])
         store_words(slice(0, chunks[2].stop))

@@ -229,17 +229,18 @@ def tile_picked_moe2w_relu_po_kernel(
         def store_words(cols):
             nc.sync.dma_start(out_words[:, cols], o_codes[:, cols].bitcast(I32))
 
-        res = [keep.tile([P, PACK, CHUNK], F32, name="res%d" % c, align_bytes=ALIGN) for c in range(len(chunks))]
+        res = [keep.tile([P, PACK, CHUNK], F32, name="res%d" % c, align_bytes=ALIGN) for c in range(2)]
+        res_late = keep.tile([P, PACK, 2 * CHUNK], F32, name="res_late", align_bytes=ALIGN)
+        res.extend((res_late[:, :, :CHUNK], res_late[:, :, CHUNK:]))
         nc.vector.tensor_copy(res[0][:, :2], acc0_lo[:])
         nc.scalar.copy(res[0][:, 2:], acc0_hi[:])
         nc.sync.dma_start(out_rows[:, :, chunks[0]], res[0][:])
         nc.scalar.copy(res[1][:], acc1[:])
         nc.sync.dma_start(out_rows[:, :, chunks[1]], res[1][:])
         nc.scalar.copy(res[2][:], acc2[:])
-        nc.sync.dma_start(out_rows[:, :, chunks[2]], res[2][:])
         nc.vector.tensor_copy(res[3][:, :2], acc3_lo[:])
         nc.scalar.copy(res[3][:, 2:], acc3_hi[:])
-        nc.sync.dma_start(out_rows[:, :, chunks[3]], res[3][:])
+        nc.sync.dma_start(out_rows[:, :, halves[1]], res_late[:])
         interleave(chunks[0], res[0][:], nc.vector.tensor_copy)
         interleave(chunks[1], res[1][:], nc.vector.tensor_copy)
         quantize_out(halves[0])

@@ -229,27 +229,24 @@ def tile_picked_moe2w_relu_po_kernel(
         def store_words(cols):
             nc.sync.dma_start(out_words[:, cols], o_codes[:, cols].bitcast(I32))
 
-        res = [keep.tile([P, PACK, CHUNK], F32, name="res%d" % c, align_bytes=ALIGN) for c in range(2)]
-        res_late = keep.tile([P, PACK, 2 * CHUNK], F32, name="res_late", align_bytes=ALIGN)
-        res.extend((res_late[:, :, :CHUNK], res_late[:, :, CHUNK:]))
-        nc.vector.tensor_copy(res[0][:, :2], acc0_lo[:])
+        res_first = keep.tile([P, PACK, CHUNK], F32, name="res_first", align_bytes=ALIGN)
+        res_rest = keep.tile([P, PACK, S - CHUNK], F32, name="res_rest", align_bytes=ALIGN)
+        res = [res_first[:]] + [res_rest[:, :, c : c + CHUNK] for c in range(0, S - CHUNK, CHUNK)]
+        nc.scalar.copy(res[0][:, :2], acc0_lo[:])
         nc.scalar.copy(res[0][:, 2:], acc0_hi[:])
-        nc.sync.dma_start(out_rows[:, :, chunks[0]], res[0][:])
-        nc.scalar.copy(res[1][:], acc1[:])
-        nc.sync.dma_start(out_rows[:, :, chunks[1]], res[1][:])
-        nc.scalar.copy(res[2][:], acc2[:])
+        nc.sync.dma_start(out_rows[:, :, chunks[0]], res[0])
+        nc.vector.tensor_copy(res[1], acc1[:])
+        nc.scalar.copy(res[2], acc2[:])
         nc.vector.tensor_copy(res[3][:, :2], acc3_lo[:])
         nc.scalar.copy(res[3][:, 2:], acc3_hi[:])
-        nc.sync.dma_start(out_rows[:, :, halves[1]], res_late[:])
-        interleave(chunks[0], res[0][:], nc.vector.tensor_copy)
-        interleave(chunks[1], res[1][:], nc.vector.tensor_copy)
-        quantize_out(halves[0])
+        nc.sync.dma_start(out_rows[:, :, CHUNK:], res_rest[:])
+        interleave(chunks[0], res[0], nc.vector.tensor_copy)
+        interleave(chunks[1], res[1], nc.vector.tensor_copy)
         interleave(chunks[2], acc2[:], nc.scalar.copy)
-        interleave(chunks[3], res[3][:], nc.vector.tensor_copy)
-        quantize_out(chunks[2])
-        store_words(slice(0, chunks[2].stop))
-        quantize_out(chunks[3])
-        store_words(chunks[3])
+        interleave(chunks[3], res[3], nc.scalar.copy)
+        quantize_out(halves[0])
+        quantize_out(halves[1])
+        store_words(slice(0, S))
         for q in range(4):
             queue = nc.scalar if q == 0 else nc.sync
             queue.dma_start(out_2[0, 4 * q : 4 * q + 4, :].bitcast(I32), o_sc[QUADRANT * q : QUADRANT * q + 4, :].bitcast(I32))

@@ -52,7 +52,7 @@ def tile_picked_moe2w_relu_po_kernel(
         xs_all = w_pool.tile([P, T], U8, name="xs_all", align_bytes=ALIGN, offset=2 * N)
         xs = keep.tile([P, S], U8, name="xs", align_bytes=ALIGN)
         xw_all = xw_pool.tile([P, T], U32, name="xw_all", align_bytes=ALIGN, offset=0)
-        w1_raw = keep.tile([P, PACK, H], F32, name="w1_raw", align_bytes=ALIGN)
+        w1_raw = d_pool.tile([P, PACK, H], F32, name="w1_raw", align_bytes=ALIGN, offset=0)
         w3s_raw = keep.tile([P, N], U8, name="w3s_raw", align_bytes=ALIGN)
 
         def move_to_plane(plane, rows, rows_at, count):
@@ -84,14 +84,14 @@ def tile_picked_moe2w_relu_po_kernel(
                 raw[:].rearrange("p j (m t) -> p m j t", t=PACK)[:, ms, :, ts],
             )
 
-        w1_dealt = d_pool.tile([P, PACK * H], BF16, name="w1_dealt", align_bytes=ALIGN, offset=0)
+        w1_dealt = keep.tile([P, PACK * H], BF16, name="w1_dealt", align_bytes=ALIGN)
         w1_codes = keep.tile([P, H], U32, name="w1_codes", align_bytes=ALIGN)
-        w1_sc = keep.tile([P, H], U8, name="w1_sc", align_bytes=ALIGN)
+        w1_sc0 = keep.tile([P, H // 2], U8, name="w1_sc0", align_bytes=ALIGN)
         w2_sc = [keep.tile([P, H // 2], U8, name="w2_sc%d" % u, align_bytes=ALIGN) for u in range(2)]
 
         deal_weights(w1_raw, w1_dealt, slice(0, W1_SHARE), slice(0, PACK), nc.scalar.copy)
         deal_weights(w1_raw, w1_dealt, slice(W1_SHARE, P), slice(0, PACK), nc.vector.tensor_copy)
-        nc.vector.quantize_mx(w1_codes[:].bitcast(FP8X4), w1_sc[:], w1_dealt[:])
+        nc.vector.quantize_mx(w1_codes[:, : H // 2].bitcast(FP8X4), w1_sc0[:], w1_dealt[:, : 2 * H])
 
         w3w_raw = w_pool.tile([P, 2 * N], U8, name="w3w_raw", align_bytes=ALIGN, offset=ALIGN)
         wa_t = w_pool.tile([P, V], F32, name="wa_t", align_bytes=ALIGN, offset=ALIGN + 2 * N)
@@ -106,6 +106,8 @@ def tile_picked_moe2w_relu_po_kernel(
         pieces = (slice(0, 256), slice(256, 384), slice(384, 512))
         for tokens in pieces:
             nc.vector.tensor_copy(xw[:, tokens], xw_all[:].indirect(offs_t[:, tokens.start // 16 : tokens.stop // 16]))
+        w1_sc1 = xw_pool.tile([P, H // 2], U8, name="w1_sc1", align_bytes=ALIGN, offset=2 * ROW)
+        nc.vector.quantize_mx(w1_codes[:, H // 2 :].bitcast(FP8X4), w1_sc1[:], w1_dealt[:, 2 * H :])
         wb_t = xw_pool.tile([P, V], F32, name="wb_t", align_bytes=ALIGN, offset=0)
         nc.sync.dma_start(wb_t[:], wb.rearrange("(p j) v -> p j v", j=PACK)[:, 0, :])
 
@@ -133,9 +135,9 @@ def tile_picked_moe2w_relu_po_kernel(
             nc.vector.tensor_tensor(z[t][:].indirect(idx[:]), picked[:], weight[:], MULT)
 
         relu_y0 = y_pool.tile([P, S], F32, name="relu_y0", align_bytes=ALIGN, offset=0)
-        first_layer(w1_codes, w1_sc, 0, relu_y0, pieces[0])
-        first_layer(w1_codes, w1_sc, 0, relu_y0, pieces[1])
-        first_layer(w1_codes, w1_sc, 0, relu_y0, pieces[2], vector_relu, chain)
+        first_layer(w1_codes, w1_sc0, 0, relu_y0, pieces[0])
+        first_layer(w1_codes, w1_sc0, 0, relu_y0, pieces[1])
+        first_layer(w1_codes, w1_sc0, 0, relu_y0, pieces[2], vector_relu, chain)
         w2_dealt0 = xw_pool.tile([P, PACK * H // 2], BF16, name="w2_dealt0", align_bytes=ALIGN, offset=4 * V)
         deal_weights(w2_raw, w2_dealt0, slice(0, P), slice(0, 2), nc.vector.tensor_copy)
         look_up_and_put("a0", relu_y0, la_t, wa_t, 0)
@@ -146,8 +148,8 @@ def tile_picked_moe2w_relu_po_kernel(
         nc.vector.quantize_mx(w2_codes[0][:].bitcast(FP8X4), w2_sc[0][:], w2_dealt0[:])
         relu_y1 = e_pool.tile([P, S], F32, name="relu_y1", align_bytes=ALIGN, offset=0)
         relu_y2 = y_pool.tile([P, S], F32, name="relu_y2", align_bytes=ALIGN, offset=ROW // 2)
-        first_layer(w1_codes, w1_sc, 1, relu_y1, banks=chain)
-        first_layer(w1_codes, w1_sc, 2, relu_y2)
+        first_layer(w1_codes, w1_sc0, 1, relu_y1, banks=chain)
+        first_layer(w1_codes[:, H // 2 :], w1_sc1, 0, relu_y2)
         look_up_and_put("a1", relu_y1, la_t, wa_t, 1)
         look_up_and_put("a2", relu_y2, la_t, wa_t, 2)
         w2_dealt1 = e_pool.tile([P, PACK * H // 2], BF16, name="w2_dealt1", align_bytes=ALIGN, offset=0)
@@ -159,7 +161,7 @@ def tile_picked_moe2w_relu_po_kernel(
         look_up_and_put("b0", relu_e[0], lb_t, wb_t, 0)
         first_layer(w2_codes[0], w2_sc[0], 1, relu_e[1])
         relu_y3 = e_pool.tile([P, S], F32, name="relu_y3", align_bytes=ALIGN, offset=ROW)
-        first_layer(w1_codes, w1_sc, 3, relu_y3)
+        first_layer(w1_codes[:, H // 2 :], w1_sc1, 1, relu_y3)
         look_up_and_put("b1", relu_e[1], lb_t, wb_t, 1)
         look_up_and_put("a3", relu_y3, la_t, wa_t, 3)
         first_layer(w2_codes[1], w2_sc[1], 0, relu_e[2])
@@ -176,7 +178,7 @@ def tile_picked_moe2w_relu_po_kernel(
         warm = chain.tile([32, S], F32, name="acc", tag="acc")
         for i in range(4):
             nc.tensor.matmul_mx(
-                warm[:], w1_codes[:, :32].bitcast(FP8X4), w3s[:, :32], w1_codes[:].bitcast(FP8X4), w1_sc[:], start=True, stop=True
+                warm[:], w1_codes[:, :32].bitcast(FP8X4), w1_sc0[:, :32], w1_codes[:].bitcast(FP8X4), w3s[:], start=True, stop=True
             )
         z_rows = e_pool.tile([P, PACK - 1, S], BF16, name="z_rows", align_bytes=ALIGN, offset=4 * ROW)
         for t in range(PACK - 1):

from contextlib import ExitStack

import concourse.mybir as mybir

K, T, S, V, N, H = 512, 2048, 512, 256, 512, 512
FLOPS = 2 * K * H * S * 2 + 2 * H * N * S

F32 = mybir.dt.float32
BF16 = mybir.dt.bfloat16
I32 = mybir.dt.int32
U32 = mybir.dt.uint32
U16 = mybir.dt.uint16
U8 = mybir.dt.uint8
FP8X4 = mybir.dt.float8_e4m3fn_x4
FP4X4 = mybir.dt.float4_e2m1fn_x4
RELU = mybir.ActivationFunctionType.Relu
COPY = mybir.ActivationFunctionType.Copy
MULT = mybir.AluOpType.mult

P = 128
PACK = 4
BLOCKS = 16
QUADRANT = 32
CHUNK = 128
ALIGN = 64
ROW = 4 * S
X_ROWS_AT = P - BLOCKS
W3_ROWS_AT = P // 2 - BLOCKS
W1_SHARE = 44


def tile_picked_moe2w_relu_po_kernel(
    tc, x_words, x_scales, w1, w2, wa, wb, w3_words, w3_scales, offs, la, lb, out_0, out_1, out_2
):
    nc = tc.nc
    with ExitStack() as ctx:
        lists = ctx.enter_context(tc.tile_pool(name="lists", bufs=1))
        keep = ctx.enter_context(tc.tile_pool(name="keep", bufs=1))
        w_pool = ctx.enter_context(tc.tile_pool(name="w_pool", bufs=1))
        xw_pool = ctx.enter_context(tc.tile_pool(name="xw_pool", bufs=1))
        d_pool = ctx.enter_context(tc.tile_pool(name="d_pool", bufs=1))
        e_pool = ctx.enter_context(tc.tile_pool(name="e_pool", bufs=1))
        y_pool = ctx.enter_context(tc.tile_pool(name="y_pool", bufs=1))
        z_pool = ctx.enter_context(tc.tile_pool(name="z_pool", bufs=1))
        psum = ctx.enter_context(tc.psum_pool(name="psum", bufs=7))
        chain = ctx.enter_context(tc.psum_pool(name="chain", bufs=1))

        offs_t = lists.tile([P, S // 16], U16, name="offs_t")
        la_t = lists.tile([P, V // 16], U16, name="la_t")
        lb_t = lists.tile([P, V // 16], U16, name="lb_t")

        xs_all = w_pool.tile([P, T], U8, name="xs_all", align_bytes=ALIGN, offset=2 * N)
        xs = keep.tile([P, S], U8, name="xs", align_bytes=ALIGN)
        xw_all = xw_pool.tile([P, T], U32, name="xw_all", align_bytes=ALIGN, offset=0)
        w1_raw = d_pool.tile([P, PACK, H], F32, name="w1_raw", align_bytes=ALIGN, offset=0)
        w3s_raw = keep.tile([P, N], U8, name="w3s_raw", align_bytes=ALIGN)

        def move_to_plane(plane, rows, rows_at, count):
            for q in range(4):
                first = rows_at + 4 * q
                nc.sync.dma_start(plane[QUADRANT * q : QUADRANT * q + count, :].bitcast(I32), rows[first : first + count, :].bitcast(I32))

        nc.vector.memset(xs_all[:X_ROWS_AT, :].bitcast(I32), 0)
        nc.vector.memset(w3s_raw[:W3_ROWS_AT, :].bitcast(I32), 0)
        nc.vector.memset(w3s_raw[P // 2 :, :].bitcast(I32), 0)
        nc.vector.memset(xs[:].bitcast(I32), 0)
        nc.sync.dma_start(xs_all[X_ROWS_AT:, :].bitcast(I32), x_scales[0].bitcast(I32))
        nc.sync.dma_start(offs_t[:], offs)
        nc.scalar.dma_start(w3s_raw[W3_ROWS_AT : P // 2, :].bitcast(I32), w3_scales[0].bitcast(I32))
        nc.sync.dma_start(w1_raw[:], w1.rearrange("(p j) h -> p j h", j=PACK))
        nc.sync.dma_start(xw_all[:].bitcast(I32), x_words[0].rearrange("p c r -> p (c r)").bitcast(I32))
        nc.sync.dma_start(la_t[:], la)
        nc.sync.dma_start(lb_t[:], lb)

        xs_rows = keep.tile([P, S], U8, name="xs_rows", align_bytes=ALIGN)
        nc.vector.tensor_copy(xs_rows[:], xs_all[:].indirect(offs_t[:]))
        move_to_plane(xs, xs_rows, X_ROWS_AT, 4)
        w3s_rows = keep.tile([P, N], U8, name="w3s_rows", align_bytes=ALIGN)
        nc.vector.tensor_copy(w3s_rows[:].rearrange("p (t m) -> p t m", t=PACK), w3s_raw[:].rearrange("p (m t) -> p t m", t=PACK))

        def deal_weights(raw, dealt, ms, ts, copy):
            copy(
                dealt[:].rearrange("p (t m j) -> p m j t", m=P, j=PACK)[:, ms],
                raw[:].rearrange("p j (m t) -> p m j t", t=PACK)[:, ms, :, ts],
            )

        w1_dealt = keep.tile([P, PACK * H], BF16, name="w1_dealt", align_bytes=ALIGN)
        w1_codes = keep.tile([P, H], U32, name="w1_codes", align_bytes=ALIGN)
        w1_sc0 = keep.tile([P, H // 2], U8, name="w1_sc0", align_bytes=ALIGN)
        w2_sc = [keep.tile([P, H // 2], U8, name="w2_sc%d" % u, align_bytes=ALIGN) for u in range(2)]

        deal_weights(w1_raw, w1_dealt, slice(0, W1_SHARE), slice(0, PACK), nc.scalar.copy)
        deal_weights(w1_raw, w1_dealt, slice(W1_SHARE, P), slice(0, PACK), nc.vector.tensor_copy)
        nc.vector.quantize_mx(w1_codes[:, : H // 2].bitcast(FP8X4), w1_sc0[:], w1_dealt[:, : 2 * H])

        w3w_raw = w_pool.tile([P, 2 * N], U8, name="w3w_raw", align_bytes=ALIGN, offset=ALIGN)
        wa_t = w_pool.tile([P, V], F32, name="wa_t", align_bytes=ALIGN, offset=ALIGN + 2 * N)
        w2_at = ALIGN + 2 * N + 4 * V
        w2_raw = w_pool.tile([P, PACK, H], F32, name="w2_raw", align_bytes=ALIGN, offset=w2_at)
        nc.sync.dma_start(w2_raw[:], w2.rearrange("(p j) h -> p j h", j=PACK))
        nc.sync.dma_start(wa_t[:], wa.rearrange("(p j) v -> p j v", j=PACK)[:, 0, :])
        nc.sync.dma_start(w3w_raw[:].bitcast(I32), w3_words[0].bitcast(I32))

        halves = (slice(0, S // 2), slice(S // 2, S))
        xw = d_pool.tile([P, S], U32, name="xw", align_bytes=ALIGN, offset=0)
        pieces = (slice(0, 256), slice(256, 384), slice(384, 512))
        for tokens in pieces:
            nc.vector.tensor_copy(xw[:, tokens], xw_all[:].indirect(offs_t[:, tokens.start // 16 : tokens.stop // 16]))
        w1_sc1 = xw_pool.tile([P, H // 2], U8, name="w1_sc1", align_bytes=ALIGN, offset=2 * ROW)
        nc.vector.quantize_mx(w1_codes[:, H // 2 :].bitcast(FP8X4), w1_sc1[:], w1_dealt[:, 2 * H :])
        wb_t = xw_pool.tile([P, V], F32, name="wb_t", align_bytes=ALIGN, offset=0)
        nc.sync.dma_start(wb_t[:], wb.rearrange("(p j) v -> p j v", j=PACK)[:, 0, :])

        def scalar_relu(dst, acc):
            nc.scalar.activation(dst, acc, RELU)

        def vector_relu(dst, acc):
            nc.vector.tensor_scalar_max(dst, acc, 0.0)

        def first_layer(codes, scales, index, dst, tokens=slice(0, S), relu=scalar_relu, banks=psum):
            cols = slice(index * P, (index + 1) * P)
            acc = banks.tile([P, tokens.stop - tokens.start], F32, name="acc", tag="acc")
            nc.tensor.matmul_mx(
                acc[:], codes[:, cols].bitcast(FP8X4), scales[:, cols], xw[:, tokens].bitcast(FP8X4), xs[:, tokens], start=True, stop=True
            )
            relu(dst[:, tokens], acc[:])

        z = [keep.tile([P, S], F32, name="z%d" % t, align_bytes=ALIGN) for t in range(2)]
        z.append(z_pool.tile([P, S], F32, name="z2", align_bytes=ALIGN, offset=0))
        z.append(keep.tile([P, S], F32, name="z3", align_bytes=ALIGN))

        def look_up_and_put(name, src, idx, weight, t):
            picked = keep.tile([P, V], F32, name=name, align_bytes=ALIGN)
            nc.scalar.activation(picked[:], src[:].indirect(idx[:]), COPY)
            nc.vector.tensor_tensor(z[t][:].indirect(idx[:]), picked[:], weight[:], MULT)

        relu_y0 = y_pool.tile([P, S], F32, name="relu_y0", align_bytes=ALIGN, offset=0)
        first_layer(w1_codes, w1_sc0, 0, relu_y0, pieces[0])
        first_layer(w1_codes, w1_sc0, 0, relu_y0, pieces[1])
        first_layer(w1_codes, w1_sc0, 0, relu_y0, pieces[2], vector_relu, chain)
        w2_dealt0 = xw_pool.tile([P, PACK * H // 2], BF16, name="w2_dealt0", align_bytes=ALIGN, offset=4 * V)
        deal_weights(w2_raw, w2_dealt0, slice(0, P), slice(0, 2), nc.vector.tensor_copy)
        look_up_and_put("a0", relu_y0, la_t, wa_t, 0)
        w2_codes = [
            y_pool.tile([P, H // 2], U32, name="w2_codes0", align_bytes=ALIGN, offset=0),
            keep.tile([P, H // 2], U32, name="w2_codes1", align_bytes=ALIGN),
        ]
        nc.vector.quantize_mx(w2_codes[0][:].bitcast(FP8X4), w2_sc[0][:], w2_dealt0[:])
        relu_y1 = e_pool.tile([P, S], F32, name="relu_y1", align_bytes=ALIGN, offset=0)
        relu_y2 = y_pool.tile([P, S], F32, name="relu_y2", align_bytes=ALIGN, offset=ROW // 2)
        first_layer(w1_codes, w1_sc0, 1, relu_y1, banks=chain)
        first_layer(w1_codes[:, H // 2 :], w1_sc1, 0, relu_y2)
        look_up_and_put("a1", relu_y1, la_t, wa_t, 1)
        look_up_and_put("a2", relu_y2, la_t, wa_t, 2)
        w2_dealt1 = e_pool.tile([P, PACK * H // 2], BF16, name="w2_dealt1", align_bytes=ALIGN, offset=0)
        relu_e = [e_pool.tile([P, S], F32, name="relu_e%d" % t, align_bytes=ALIGN, offset=ROW * (1 + t)) for t in range(PACK)]
        deal_weights(w2_raw, w2_dealt1, slice(0, P // 2), slice(2, 4), nc.scalar.copy)
        first_layer(w2_codes[0], w2_sc[0], 0, relu_e[0])
        deal_weights(w2_raw, w2_dealt1, slice(P // 2, P), slice(2, 4), nc.scalar.copy)
        nc.vector.quantize_mx(w2_codes[1][:].bitcast(FP8X4), w2_sc[1][:], w2_dealt1[:])
        look_up_and_put("b0", relu_e[0], lb_t, wb_t, 0)
        first_layer(w2_codes[0], w2_sc[0], 1, relu_e[1])
        relu_y3 = e_pool.tile([P, S], F32, name="relu_y3", align_bytes=ALIGN, offset=ROW)
        first_layer(w1_codes[:, H // 2 :], w1_sc1, 1, relu_y3)
        look_up_and_put("b1", relu_e[1], lb_t, wb_t, 1)
        look_up_and_put("a3", relu_y3, la_t, wa_t, 3)
        first_layer(w2_codes[1], w2_sc[1], 0, relu_e[2])
        first_layer(w2_codes[1], w2_sc[1], 1, relu_e[3])
        look_up_and_put("b2", relu_e[2], lb_t, wb_t, 2)
        look_up_and_put("b3", relu_e[3], lb_t, wb_t, 3)
        w3w = e_pool.tile([P, 2 * N], U8, name="w3w", align_bytes=ALIGN, offset=2 * ROW)
        nc.scalar.copy(
            w3w[:].bitcast(U16).rearrange("p (t m) -> p t m", t=PACK), w3w_raw[:].bitcast(U16).rearrange("p (m t) -> p t m", t=PACK)
        )

        w3s = w_pool.tile([P, N], U8, name="w3s", align_bytes=ALIGN, offset=ALIGN)
        move_to_plane(w3s, w3s_rows, W3_ROWS_AT, QUADRANT)
        warm = chain.tile([32, S], F32, name="acc", tag="acc")
        for i in range(4):
            nc.tensor.matmul_mx(
                warm[:], w1_codes[:, :32].bitcast(FP8X4), w1_sc0[:, :32], w1_codes[:].bitcast(FP8X4), w3s[:], start=True, stop=True
            )
        z_rows = e_pool.tile([P, PACK - 1, S], BF16, name="z_rows", align_bytes=ALIGN, offset=4 * ROW)
        for t in range(PACK - 1):
            nc.scalar.copy(z_rows[:, t, :], z[t][:])
        z_bf = z_pool.tile([P, S, PACK], BF16, name="z_bf", align_bytes=ALIGN, offset=0)
        nc.scalar.copy(z_bf[:, halves[1], 0:3], z_rows[:, :, halves[1]].rearrange("p t s -> p s t"))

        z_codes = keep.tile([P, S], U32, name="z_codes", align_bytes=ALIGN)
        z_sc = keep.tile([P, S], U8, name="z_sc", align_bytes=ALIGN)
        o_codes = keep.tile([P, S], U32, name="o_codes", align_bytes=ALIGN)
        o_sc = keep.tile([P, S], U8, name="o_sc", align_bytes=ALIGN)
        out_rows = out_0.rearrange("(p t) s -> p t s", t=PACK)
        out_words = out_1[0].rearrange("p c r -> p (c r)").bitcast(I32)
        chunks = [slice(c, c + CHUNK) for c in range(0, S, CHUNK)]
        for cols in chunks:
            if cols.stop <= halves[0].stop:
                nc.vector.tensor_copy(z_bf[:, cols, 0:3], z_rows[:, :, cols].rearrange("p t s -> p s t"))
                nc.vector.tensor_copy(z_bf[:, cols, 3], z[3][:, cols])
            else:
                nc.scalar.copy(z_bf[:, cols, 3], z[3][:, cols])
            nc.vector.quantize_mx(z_codes[:, cols].bitcast(FP8X4), z_sc[:, cols], z_bf[:, cols, :].rearrange("p s t -> p (s t)"))
        res_bf = keep.tile([P, S, PACK], BF16, name="res_bf", align_bytes=ALIGN)

        def second_layer(cols, tiles):
            acc = psum.tile([P, len(tiles), CHUNK], F32, name="acc", tag="acc")
            for i, t in enumerate(tiles):
                nc.tensor.matmul_mx(
                    acc[:, i, :],
                    w3w[:, 2 * P * t : 2 * P * (t + 1)].bitcast(FP4X4),
                    w3s[:, P * t : P * (t + 1)],
                    z_codes[:, cols].bitcast(FP8X4),
                    z_sc[:, cols],
                    start=True,
                    stop=True,
                )
            return acc

        acc0_lo = second_layer(chunks[0], (0, 1))
        acc0_hi = second_layer(chunks[0], (2, 3))
        acc1, acc2 = [second_layer(cols, range(PACK)) for cols in chunks[1:3]]
        acc3_lo = second_layer(chunks[3], (0, 1))
        acc3_hi = second_layer(chunks[3], (2, 3))

        def interleave(cols, res, copy):
            copy(res_bf[:, cols, :].rearrange("p (s i) t -> p s t i", i=4), res.rearrange("p t (s i) -> p s t i", i=4))

        def quantize_out(cols):
            nc.vector.quantize_mx(o_codes[:, cols].bitcast(FP8X4), o_sc[:, cols], res_bf[:, cols, :].rearrange("p s t -> p (s t)"))

        def store_words(cols):
            nc.sync.dma_start(out_words[:, cols], o_codes[:, cols].bitcast(I32))

        res_first = keep.tile([P, PACK, CHUNK], F32, name="res_first", align_bytes=ALIGN)
        res_rest = keep.tile([P, PACK, S - CHUNK], F32, name="res_rest", align_bytes=ALIGN)
        res = [res_first[:]] + [res_rest[:, :, c : c + CHUNK] for c in range(0, S - CHUNK, CHUNK)]
        nc.scalar.copy(res[0][:, :2], acc0_lo[:])
        nc.scalar.copy(res[0][:, 2:], acc0_hi[:])
        nc.sync.dma_start(out_rows[:, :, chunks[0]], res[0])
        nc.vector.tensor_copy(res[1], acc1[:])
        nc.scalar.copy(res[2], acc2[:])
        nc.vector.tensor_copy(res[3][:, :2], acc3_lo[:])
        nc.scalar.copy(res[3][:, 2:], acc3_hi[:])
        nc.sync.dma_start(out_rows[:, :, CHUNK:], res_rest[:])
        interleave(chunks[0], res[0], nc.vector.tensor_copy)
        interleave(chunks[1], res[1], nc.vector.tensor_copy)
        interleave(chunks[2], acc2[:], nc.scalar.copy)
        interleave(chunks[3], res[3], nc.scalar.copy)
        quantize_out(halves[0])
        quantize_out(halves[1])
        store_words(slice(0, S))
        for q in range(4):
            queue = nc.scalar if q == 0 else nc.sync
            queue.dma_start(out_2[0, 4 * q : 4 * q + 4, :].bitcast(I32), o_sc[QUADRANT * q : QUADRANT * q + 4, :].bitcast(I32))
